import numpy as np
import ml_dtypes


def mxq(x, axis, fmt="e4m3"):
    dtype, down = {"e4m3": (ml_dtypes.float8_e4m3fn, 7), "e5m2": (ml_dtypes.float8_e5m2, 14)}[fmt]
    v = np.moveaxis(np.asarray(x, np.float32).astype(ml_dtypes.bfloat16).astype(np.float64), axis, -1)
    blocks = v.reshape(v.shape[:-1] + (-1, 32))
    amax = np.abs(blocks).max(-1, keepdims=True)
    byte = np.maximum(np.where(amax > 0, np.frexp(amax)[1] - 1 + 127, 0) - down, 1)
    scale = np.exp2(byte - 127.0)
    codes = (blocks / scale).astype(np.float32).astype(dtype).astype(np.float64)
    return np.moveaxis((codes * scale).reshape(v.shape), -1, axis)


WIDE = False


def mx_kscale(k):
    if not WIDE:
        return np.ones(k)
    levels = np.array([18, -18])
    if k % 512:
        return np.exp2(np.random.permutation(np.resize(levels, k // 32))).repeat(32)
    a = np.empty((k // 512, 16))
    for p in range(k // 512):
        a[p, :8] = np.random.permutation(np.resize(levels, 8))
        for g in range(8):
            far = levels[np.abs(levels - a[p, g]) >= 10]
            a[p, g + 8] = far[np.random.randint(len(far))]
    return np.exp2(a.ravel()).repeat(32)


def f64(x):
    return np.asarray(x).astype(np.float64)


def striped(idx):
    return np.tile(np.asarray(idx).reshape(-1, 16).T, (8, 1)).astype(np.uint16)


def unstriped(offs):
    return offs[:16].T.reshape(-1).astype(np.int64)


B, N, T, D, R = 1, 512, 2048, 512, 512


def setup_inputs():
    n = np.random.standard_normal
    idx = np.random.permutation(T)[:B * N]
    s = mx_kscale(D)[:, None]
    u = np.ones(T)
    u[idx] = mx_kscale(B * N)
    r = np.random.uniform(0.5, 2.0, T) * u
    x = n((B, D, R))
    return {
        "xT": (x * s).astype(np.float32),
        "wT": (n((D, T)) * (1.00 / np.sqrt(D)) / s / r).astype(np.float32),
        "y": n((B, R, N)).astype(np.float32),
        "wt": (np.random.uniform(0.5, 1.5, (B, R, 1)) * 1.0 / np.sqrt(R)).astype(np.float32),
        "ts": np.tile(r, (128, 1)).astype(np.float32),
        "offs": striped(idx),
    }


def reference(xT, wT, y, wt, ts, offs):
    idx = unstriped(offs)
    pick = lambda x: x[:, idx].reshape(x.shape[0], B, N).transpose(1, 0, 2)
    w = pick(f64(wT))
    a = mxq(f64(xT), 1, "e4m3").transpose(0, 2, 1) @ mxq(w, 1, "e4m3")
    ts_ = pick(f64(ts))[:, :1, :]
    a = a * ts_
    g = f64(wt) * (a - f64(y))
    g = g * ts_
    gx = mxq(g, 2, "e5m2") @ mxq(w, 2, "e4m3").transpose(0, 2, 1)
    return gx

@@ -1,0 +1,256 @@
+from contextlib import ExitStack
+
+import concourse.mybir as mybir
+from concourse.masks import make_identity
+
+F32 = mybir.dt.float32
+BF16 = mybir.dt.bfloat16
+U32 = mybir.dt.uint32
+U16 = mybir.dt.uint16
+U8 = mybir.dt.uint8
+E4M3 = mybir.dt.float8_e4m3fn_x4
+E5M2 = mybir.dt.float8_e5m2_x4
+MULT = mybir.AluOpType.mult
+COPY = mybir.ActivationFunctionType.Copy
+
+P = 128
+PACK = 4
+SLOTS = 512
+ITEMS = 2048
+FEATURES = 512
+ROWS = 512
+ROW_TILES = ROWS // P
+TILES_PER_LOAD = 2
+
+TABLE_BYTES = 4 * ITEMS
+
+FLOPS = 2 * 2 * ROWS * SLOTS * FEATURES
+
+
+def tile_attend_gsq_x_ts_kernel(tc, xT, wT, y, wt, ts, offs, out):
+    nc = tc.nc
+    with ExitStack() as ctx:
+        keep = ctx.enter_context(tc.tile_pool(name="keep", bufs=1))
+        reuse = ctx.enter_context(tc.tile_pool(name="reuse", bufs=1))
+        psum = ctx.enter_context(tc.psum_pool(name="psum", bufs=2))
+
+        offsets = keep.tile([P, SLOTS // 16], U16, name="offsets")
+        nc.sync.dma_start(offsets[:], offs)
+
+        ts_folded = reuse.tile([P, ITEMS // P], F32, name="ts_folded", offset=3 * TABLE_BYTES)
+        nc.scalar.dma_start(out=ts_folded[:], in_=ts[0].rearrange("(n c) -> n c", n=P))
+        wt_cols = keep.tile([P, ROW_TILES], F32, name="wt_cols")
+        nc.scalar.dma_start(
+            out=wt_cols[:].rearrange("p (h jj) -> p h jj", jj=TILES_PER_LOAD),
+            in_=wt[0].rearrange("(h p jj) o -> p h (jj o)", p=P, jj=TILES_PER_LOAD),
+        )
+
+        ident_f32 = keep.tile([P, P], F32, name="ident_f32")
+        make_identity(nc, ident_f32[:])
+        ident_bf16 = keep.tile([P, P], BF16, name="ident_bf16")
+        make_identity(nc, ident_bf16[:])
+
+        w_planes = wT.rearrange("(p t) c -> p t c", t=PACK)
+        tables = []
+        for t in range(PACK):
+            tables.append(reuse.tile([P, ITEMS], F32, name="table%d" % t, offset=t * TABLE_BYTES))
+        for t in range(PACK - 1):
+            nc.sync.dma_start(out=tables[t][:], in_=w_planes[:, t, :])
+
+        x_planes = xT[0].rearrange("(p t) r -> p t r", t=PACK)
+        y_tiles = y[0].rearrange("(h p jj) i -> h p jj i", p=P, jj=TILES_PER_LOAD)
+        out_tiles = out[0].rearrange("(h p jj) d -> h jj p d", p=P, jj=TILES_PER_LOAD)
+        x_raw = []
+        y_raw = []
+
+        def load_rows(half):
+            width = TILES_PER_LOAD * P
+            x_half = reuse.tile([P, PACK, width], F32, name="x_raw%d" % half, offset=half * TABLE_BYTES)
+            nc.sync.dma_start(out=x_half[:], in_=x_planes[:, :, half * width : (half + 1) * width])
+            y_half = reuse.tile(
+                [P, TILES_PER_LOAD, SLOTS], F32, name="y_raw%d" % half, offset=half * TABLE_BYTES + TABLE_BYTES // 2
+            )
+            nc.sync.dma_start(out=y_half[:], in_=y_tiles[half])
+            for jj in range(TILES_PER_LOAD):
+                x_raw.append(x_half[:, :, jj:width:TILES_PER_LOAD])
+                y_raw.append(y_half[:, jj, :])
+
+        ts_table = reuse.tile([P, ITEMS], F32, name="ts_table", offset=4 * TABLE_BYTES)
+        ts_quarters = ts_table[:].rearrange("p (n q c) -> p q n c", q=PACK, c=PACK)
+        for q, tag in enumerate(("early", "score", "grad", "out")):
+            spread_bank = psum.tile([P, PACK, P], F32, name="spread_bank%d" % q, tag=tag)
+            for c in range(PACK):
+                col = PACK * q + c
+                nc.tensor.transpose(spread_bank[:, c, :], ts_folded[:, col : col + 1].to_broadcast([P, P]), ident_f32[:])
+            nc.scalar.activation(out=ts_quarters[:, q, :, :], in_=spread_bank[:].rearrange("p c n -> p n c"), func=COPY)
+        nc.sync.dma_start(out=tables[PACK - 1][:], in_=w_planes[:, PACK - 1, :])
+        ts_row = keep.tile([P, SLOTS], F32, name="ts_row")
+        nc.vector.tensor_copy(out=ts_row[:], in_=ts_table[:].indirect(offsets[:]))
+        ts_spread = keep.tile([P, SLOTS], F32, name="ts_spread")
+        nc.scalar.activation(
+            out=ts_spread[:].rearrange("p (u s) -> p s u", u=PACK),
+            in_=ts_row[:].rearrange("p (s u) -> p s u", u=PACK),
+            func=COPY,
+            scale=-1.0,
+        )
+        ts_bank = psum.tile([P, PACK, P], F32, name="ts_bank", tag="grad")
+        for u in range(PACK):
+            nc.tensor.transpose(ts_bank[:, u, :], ts_spread[:, u * P : (u + 1) * P], ident_f32[:])
+        ts_cols = keep.tile([P, PACK], F32, name="ts_cols")
+        nc.scalar.copy(out=ts_cols[:], in_=ts_bank[:, :, 0])
+
+        w_by_d = reuse.tile([P, SLOTS, PACK], BF16, name="w_by_d", align_bytes=64, offset=4 * TABLE_BYTES)
+        w_dealt = w_by_d[:].rearrange("p (u s) t -> p s u t", u=PACK)
+        wn_codes = keep.tile([P, FEATURES], U32, name="wn_codes", align_bytes=64)
+        w_scales = keep.tile([P, SLOTS], U8, name="w_scales", align_bytes=64)
+        wn_scales = w_scales[:]
+        wd_scales = w_scales[4:P, :]
+        wd_codes = keep.tile([P, SLOTS], U32, name="wd_codes", align_bytes=64)
+        w_by_slot = []
+
+        def gather_plane(t):
+            nc.vector.tensor_copy(out=w_dealt[:, :, :, t], in_=tables[t][:].indirect(offsets[:]))
+
+        def turn_plane(t):
+            turn_bank = psum.tile([P, PACK, P], BF16, name="turn_bank%d" % t, tag="early")
+            for u in range(PACK):
+                nc.tensor.transpose(turn_bank[:, u, :], w_by_d[:, u * P : (u + 1) * P, t], ident_bf16[:])
+            if t == PACK - 1:
+                turned = reuse.tile([P, P, PACK], BF16, name="w_by_slot%d" % t, align_bytes=64, offset=0)
+            else:
+                turned = keep.tile([P, P, PACK], BF16, name="w_by_slot%d" % t, align_bytes=64)
+            nc.scalar.copy(out=turned[:], in_=turn_bank[:].rearrange("s u p -> s p u"))
+            w_by_slot.append(turned)
+
+        def quantise_turned(t):
+            cols = slice(t * P, (t + 1) * P)
+            nc.vector.quantize_mx(
+                out=wn_codes[:, cols].bitcast(E4M3),
+                scales=wn_scales[:, cols],
+                in_=w_by_slot[t][:].rearrange("s p u -> s (p u)"),
+            )
+
+        for t in range(PACK - 1):
+            gather_plane(t)
+            if t < 2:
+                load_rows(t)
+            turn_plane(t)
+            if t < 2:
+                quantise_turned(t)
+        gather_plane(PACK - 1)
+        nc.vector.quantize_mx(out=wd_codes[:].bitcast(E4M3), scales=wd_scales, in_=w_by_d[:].rearrange("p c t -> p (c t)"))
+        quantise_turned(2)
+
+        x_codes = []
+        x_scales = []
+        score_bank = []
+        grad_bank = []
+        y_neg = []
+        score = {}
+        h_in = {}
+
+        def prepare(j):
+            x_in = keep.tile([P, P, PACK], BF16, name="x_in%d" % j, align_bytes=64)
+            nc.scalar.copy(
+                out=x_in[:].rearrange("p (c i) t -> p c t i", i=2),
+                in_=x_raw[j].rearrange("p t (c i) -> p c t i", i=2),
+            )
+            codes = keep.tile([P, P], U32, name="x_codes%d" % j, tag="x_codes", bufs=2, align_bytes=64)
+            scales = keep.tile([P, P], U8, name="x_scales%d" % j, align_bytes=64)
+            nc.vector.quantize_mx(out=codes[:].bitcast(E4M3), scales=scales[:], in_=x_in[:].rearrange("p c t -> p (c t)"))
+            x_codes.append(codes)
+            x_scales.append(scales)
+            bank = psum.tile([P, SLOTS], F32, name="score_bank%d" % j, tag="score")
+            nc.tensor.matmul_mx(
+                out=bank[:],
+                lhsT=codes[:].bitcast(E4M3),
+                lhsT_scale=scales[:],
+                rhs=wd_codes[:].bitcast(E4M3),
+                rhs_scale=wd_scales,
+                start=True,
+                stop=True,
+            )
+            score_bank.append(bank)
+
+        def weigh_targets(j):
+            target = keep.tile([P, PACK, P], F32, name="y_neg%d" % j)
+            nc.scalar.activation(
+                out=target[:].rearrange("r u s -> r s u"),
+                in_=y_raw[j].rearrange("r (s u) -> r s u", u=PACK),
+                func=COPY,
+                scale=wt_cols[:, j : j + 1],
+            )
+            y_neg.append(target)
+
+        def scores(j):
+            scaled = keep.tile([P, SLOTS], F32, name="score%d" % j)
+            nc.vector.scalar_tensor_tensor(
+                out=scaled[:], in0=score_bank[j][:], scalar=wt_cols[:, j : j + 1], in1=ts_spread[:], op0=MULT, op1=MULT
+            )
+            score[j] = scaled
+
+        def turn_gradient(j):
+            bank = psum.tile([P, PACK, P], F32, name="grad_bank%d" % j, tag="grad" if j < 2 else "early")
+            for u in range(PACK):
+                nc.tensor.matmul(
+                    bank[:, u, :], lhsT=y_neg[j][:, u, :], rhs=ident_f32[:], start=(u == 0), stop=False, is_transpose=True
+                )
+            for u in range(PACK):
+                nc.tensor.matmul(
+                    bank[:, u, :],
+                    lhsT=score[j][:, u * P : (u + 1) * P],
+                    rhs=ident_f32[:],
+                    start=False,
+                    stop=(u == PACK - 1),
+                    is_transpose=True,
+                )
+            grad_bank.append(bank)
+
+        def scale_gradient(j):
+            bank = grad_bank[j]
+            h_tile = keep.tile([P, P, PACK], BF16, name="h_in%d" % j, align_bytes=64)
+            nc.vector.tensor_tensor(
+                out=h_tile[:],
+                in0=bank[:].rearrange("s u r -> s r u"),
+                in1=ts_cols[:].unsqueeze(1).to_broadcast([P, P, PACK]),
+                op=MULT,
+            )
+            h_in[j] = h_tile
+
+        def finish(j):
+            codes = keep.tile([P, P], U32, name="h_codes%d" % j, align_bytes=64)
+            scales = keep.tile([P, P], U8, name="h_scales%d" % j, align_bytes=64)
+            nc.vector.quantize_mx(
+                out=codes[:].bitcast(E5M2), scales=scales[:], in_=h_in[j][:].rearrange("s r u -> s (r u)")
+            )
+            bank = psum.tile([P, FEATURES], F32, name="out_bank%d" % j, tag="out")
+            nc.tensor.matmul_mx(
+                out=bank[:],
+                lhsT=codes[:].bitcast(E5M2),
+                lhsT_scale=scales[:],
+                rhs=wn_codes[:].bitcast(E4M3),
+                rhs_scale=wn_scales,
+                start=True,
+                stop=True,
+            )
+            result = keep.tile([P, P, PACK], F32, name="result%d" % j)
+            nc.scalar.copy(out=result[:], in_=bank[:].rearrange("r (t p) -> r p t", t=PACK))
+            nc.sync.dma_start(out=out_tiles[j // TILES_PER_LOAD, j % TILES_PER_LOAD], in_=result[:].rearrange("r p t -> r (p t)"))
+
+        prepare(0)
+        prepare(1)
+        turn_plane(PACK - 1)
+        for step in range(ROW_TILES + 2):
+            if step < ROW_TILES:
+                scores(step)
+            if step == 0:
+                quantise_turned(PACK - 1)
+            if step >= 2:
+                finish(step - 2)
+            if 2 <= step + 1 < ROW_TILES:
+                prepare(step + 1)
+            if step < ROW_TILES:
+                weigh_targets(step)
+                turn_gradient(step)
+            if 1 <= step <= ROW_TILES:
+                scale_gradient(step - 1)

@@ -39,16 +39,11 @@ def tile_attend_gsq_x_ts_kernel(tc, xT, wT, y, wt, ts, offs, out):
 
         ts_folded = reuse.tile([P, ITEMS // P], F32, name="ts_folded", offset=3 * TABLE_BYTES)
         nc.scalar.dma_start(out=ts_folded[:], in_=ts[0].rearrange("(n c) -> n c", n=P))
-        wt_cols = keep.tile([P, ROW_TILES], F32, name="wt_cols")
-        nc.scalar.dma_start(
-            out=wt_cols[:].rearrange("p (h jj) -> p h jj", jj=TILES_PER_LOAD),
-            in_=wt[0].rearrange("(h p jj) o -> p h (jj o)", p=P, jj=TILES_PER_LOAD),
-        )
+        wt_rows = keep.tile([P, P], F32, name="wt_rows")
+        nc.gpsimd.memset(wt_rows[:], 0.0)
 
         ident_f32 = keep.tile([P, P], F32, name="ident_f32")
         make_identity(nc, ident_f32[:])
-        ident_bf16 = keep.tile([P, P], BF16, name="ident_bf16")
-        make_identity(nc, ident_bf16[:])
 
         w_planes = wT.rearrange("(p t) c -> p t c", t=PACK)
         tables = []
@@ -56,10 +51,11 @@ def tile_attend_gsq_x_ts_kernel(tc, xT, wT, y, wt, ts, offs, out):
             tables.append(reuse.tile([P, ITEMS], F32, name="table%d" % t, offset=t * TABLE_BYTES))
         for t in range(PACK - 1):
             nc.sync.dma_start(out=tables[t][:], in_=w_planes[:, t, :])
+            if t == 0:
+                nc.sync.dma_start(out=wt_rows[0:ROW_TILES, :], in_=wt[0].rearrange("(j p) o -> j (p o)", p=P))
 
         x_planes = xT[0].rearrange("(p t) r -> p t r", t=PACK)
-        y_tiles = y[0].rearrange("(h p jj) i -> h p jj i", p=P, jj=TILES_PER_LOAD)
-        out_tiles = out[0].rearrange("(h p jj) d -> h jj p d", p=P, jj=TILES_PER_LOAD)
+        y_tiles = y[0].rearrange("(j p) i -> p j i", p=P)
         x_raw = []
         y_raw = []
 
@@ -70,9 +66,9 @@ def tile_attend_gsq_x_ts_kernel(tc, xT, wT, y, wt, ts, offs, out):
             y_half = reuse.tile(
                 [P, TILES_PER_LOAD, SLOTS], F32, name="y_raw%d" % half, offset=half * TABLE_BYTES + TABLE_BYTES // 2
             )
-            nc.sync.dma_start(out=y_half[:], in_=y_tiles[half])
+            nc.sync.dma_start(out=y_half[:], in_=y_tiles[:, half * TILES_PER_LOAD : (half + 1) * TILES_PER_LOAD, :])
             for jj in range(TILES_PER_LOAD):
-                x_raw.append(x_half[:, :, jj:width:TILES_PER_LOAD])
+                x_raw.append(x_half[:, :, jj * P : (jj + 1) * P])
                 y_raw.append(y_half[:, jj, :])
 
         ts_table = reuse.tile([P, ITEMS], F32, name="ts_table", offset=4 * TABLE_BYTES)
@@ -99,8 +95,16 @@ def tile_attend_gsq_x_ts_kernel(tc, xT, wT, y, wt, ts, offs, out):
         ts_cols = keep.tile([P, PACK], F32, name="ts_cols")
         nc.scalar.copy(out=ts_cols[:], in_=ts_bank[:, :, 0])
 
-        w_by_d = reuse.tile([P, SLOTS, PACK], BF16, name="w_by_d", align_bytes=64, offset=4 * TABLE_BYTES)
-        w_dealt = w_by_d[:].rearrange("p (u s) t -> p s u t", u=PACK)
+        wt_bank = psum.tile([P, P], F32, name="wt_bank", tag="out")
+        nc.tensor.transpose(wt_bank[:], wt_rows[:], ident_f32[:])
+        wt_cols = keep.tile([P, ROW_TILES], F32, name="wt_cols")
+        nc.scalar.copy(out=wt_cols[:], in_=wt_bank[:, 0:ROW_TILES])
+
+        w_by_d = keep.tile([P, SLOTS, PACK], BF16, name="w_by_d", align_bytes=64)
+        pairs = [
+            reuse.tile([P, 2 * SLOTS], BF16, name="pair0", offset=4 * TABLE_BYTES),
+            reuse.tile([P, 2 * SLOTS], BF16, name="pair1", offset=4 * TABLE_BYTES + TABLE_BYTES // 2),
+        ]
         wn_codes = keep.tile([P, FEATURES], U32, name="wn_codes", align_bytes=64)
         w_scales = keep.tile([P, SLOTS], U8, name="w_scales", align_bytes=64)
         wn_scales = w_scales[:]
@@ -109,17 +113,33 @@ def tile_attend_gsq_x_ts_kernel(tc, xT, wT, y, wt, ts, offs, out):
         w_by_slot = []
 
         def gather_plane(t):
-            nc.vector.tensor_copy(out=w_dealt[:, :, :, t], in_=tables[t][:].indirect(offsets[:]))
+            plane = pairs[t // 2][:, (t % 2) * SLOTS : (t % 2 + 1) * SLOTS]
+            nc.vector.tensor_copy(out=plane, in_=tables[t][:].indirect(offsets[:]))
+
+        def weave_views(pair):
+            woven = w_by_d[:, :, 2 * pair : 2 * pair + 2].rearrange("p (c i) t -> p c t i", i=4)
+            planes = pairs[pair][:].rearrange("p (t c i) -> p c t i", t=2, i=4)
+            return woven, planes
+
+        turn_banks = []
 
         def turn_plane(t):
-            turn_bank = psum.tile([P, PACK, P], BF16, name="turn_bank%d" % t, tag="early")
-            for u in range(PACK):
-                nc.tensor.transpose(turn_bank[:, u, :], w_by_d[:, u * P : (u + 1) * P, t], ident_bf16[:])
+            words = pairs[t // 2][:].bitcast(F32)
+            first = (t % 2) * (SLOTS // 2)
+            turn_bank = psum.tile([P, 2, P], F32, name="turn_bank%d" % t, tag="early")
+            for v in range(2):
+                nc.tensor.transpose(turn_bank[:, v, :], words[:, first + v : first + SLOTS // 2 : 2], ident_f32[:])
+            turn_banks.append(turn_bank)
+
+        def copy_turned(t):
             if t == PACK - 1:
-                turned = reuse.tile([P, P, PACK], BF16, name="w_by_slot%d" % t, align_bytes=64, offset=0)
+                turned = reuse.tile([P, P * PACK], BF16, name="w_by_slot%d" % t, align_bytes=64, offset=TABLE_BYTES // 2)
             else:
-                turned = keep.tile([P, P, PACK], BF16, name="w_by_slot%d" % t, align_bytes=64)
-            nc.scalar.copy(out=turned[:], in_=turn_bank[:].rearrange("s u p -> s p u"))
+                turned = keep.tile([P, P * PACK], BF16, name="w_by_slot%d" % t, align_bytes=64)
+            nc.scalar.copy(
+                out=turned[:].bitcast(F32).rearrange("s (p v) -> s p v", v=2),
+                in_=turn_banks[t][:].rearrange("s v p -> s p v"),
+            )
             w_by_slot.append(turned)
 
         def quantise_turned(t):
@@ -127,7 +147,7 @@ def tile_attend_gsq_x_ts_kernel(tc, xT, wT, y, wt, ts, offs, out):
             nc.vector.quantize_mx(
                 out=wn_codes[:, cols].bitcast(E4M3),
                 scales=wn_scales[:, cols],
-                in_=w_by_slot[t][:].rearrange("s p u -> s (p u)"),
+                in_=w_by_slot[t][:],
             )
 
         for t in range(PACK - 1):
@@ -135,9 +155,16 @@ def tile_attend_gsq_x_ts_kernel(tc, xT, wT, y, wt, ts, offs, out):
             if t < 2:
                 load_rows(t)
             turn_plane(t)
+            copy_turned(t)
             if t < 2:
                 quantise_turned(t)
+            if t == 1:
+                woven, planes = weave_views(0)
+                nc.scalar.copy(out=woven, in_=planes)
         gather_plane(PACK - 1)
+        turn_plane(PACK - 1)
+        woven, planes = weave_views(1)
+        nc.vector.tensor_copy(out=woven, in_=planes)
         nc.vector.quantize_mx(out=wd_codes[:].bitcast(E4M3), scales=wd_scales, in_=w_by_d[:].rearrange("p c t -> p (c t)"))
         quantise_turned(2)
 
@@ -152,8 +179,8 @@ def tile_attend_gsq_x_ts_kernel(tc, xT, wT, y, wt, ts, offs, out):
         def prepare(j):
             x_in = keep.tile([P, P, PACK], BF16, name="x_in%d" % j, align_bytes=64)
             nc.scalar.copy(
-                out=x_in[:].rearrange("p (c i) t -> p c t i", i=2),
-                in_=x_raw[j].rearrange("p t (c i) -> p c t i", i=2),
+                out=x_in[:].rearrange("p (c i) t -> p c t i", i=4),
+                in_=x_raw[j].rearrange("p t (c i) -> p c t i", i=4),
             )
             codes = keep.tile([P, P], U32, name="x_codes%d" % j, tag="x_codes", bufs=2, align_bytes=64)
             scales = keep.tile([P, P], U8, name="x_scales%d" % j, align_bytes=64)
@@ -183,9 +210,14 @@ def tile_attend_gsq_x_ts_kernel(tc, xT, wT, y, wt, ts, offs, out):
             y_neg.append(target)
 
         def scores(j):
-            scaled = keep.tile([P, SLOTS], F32, name="score%d" % j)
+            scaled = keep.tile([P, PACK, P], F32, name="score%d" % j)
             nc.vector.scalar_tensor_tensor(
-                out=scaled[:], in0=score_bank[j][:], scalar=wt_cols[:, j : j + 1], in1=ts_spread[:], op0=MULT, op1=MULT
+                out=scaled[:],
+                in0=score_bank[j][:].rearrange("r (s u) -> r u s", u=PACK),
+                scalar=wt_cols[:, j : j + 1],
+                in1=ts_spread[:].rearrange("p (u s) -> p u s", u=PACK),
+                op0=MULT,
+                op1=MULT,
             )
             score[j] = scaled
 
@@ -198,7 +230,7 @@ def tile_attend_gsq_x_ts_kernel(tc, xT, wT, y, wt, ts, offs, out):
             for u in range(PACK):
                 nc.tensor.matmul(
                     bank[:, u, :],
-                    lhsT=score[j][:, u * P : (u + 1) * P],
+                    lhsT=score[j][:, u, :],
                     rhs=ident_f32[:],
                     start=False,
                     stop=(u == PACK - 1),
@@ -234,21 +266,24 @@ def tile_attend_gsq_x_ts_kernel(tc, xT, wT, y, wt, ts, offs, out):
                 stop=True,
             )
             result = keep.tile([P, P, PACK], F32, name="result%d" % j)
-            nc.scalar.copy(out=result[:], in_=bank[:].rearrange("r (t p) -> r p t", t=PACK))
-            nc.sync.dma_start(out=out_tiles[j // TILES_PER_LOAD, j % TILES_PER_LOAD], in_=result[:].rearrange("r p t -> r (p t)"))
+            if j == ROW_TILES - 1:
+                nc.vector.tensor_copy(out=result[:], in_=bank[:].rearrange("r (t p) -> r p t", t=PACK))
+            else:
+                nc.scalar.copy(out=result[:], in_=bank[:].rearrange("r (t p) -> r p t", t=PACK))
+            nc.sync.dma_start(out=out[0, j * P : (j + 1) * P, :], in_=result[:].rearrange("r p t -> r (p t)"))
 
         prepare(0)
         prepare(1)
-        turn_plane(PACK - 1)
         for step in range(ROW_TILES + 2):
             if step < ROW_TILES:
                 scores(step)
-            if step == 0:
+            if 2 <= step + 1 < ROW_TILES:
+                prepare(step + 1)
+            if step == 2:
+                copy_turned(PACK - 1)
                 quantise_turned(PACK - 1)
             if step >= 2:
                 finish(step - 2)
-            if 2 <= step + 1 < ROW_TILES:
-                prepare(step + 1)
             if step < ROW_TILES:
                 weigh_targets(step)
                 turn_gradient(step)

@@ -55,21 +55,21 @@ def tile_attend_gsq_x_ts_kernel(tc, xT, wT, y, wt, ts, offs, out):
                 nc.sync.dma_start(out=wt_rows[0:ROW_TILES, :], in_=wt[0].rearrange("(j p) o -> j (p o)", p=P))
 
         x_planes = xT[0].rearrange("(p t) r -> p t r", t=PACK)
-        y_tiles = y[0].rearrange("(j p) i -> p j i", p=P)
         x_raw = []
         y_raw = []
 
-        def load_rows(half):
+        def load_x(half):
             width = TILES_PER_LOAD * P
             x_half = reuse.tile([P, PACK, width], F32, name="x_raw%d" % half, offset=half * TABLE_BYTES)
             nc.sync.dma_start(out=x_half[:], in_=x_planes[:, :, half * width : (half + 1) * width])
-            y_half = reuse.tile(
-                [P, TILES_PER_LOAD, SLOTS], F32, name="y_raw%d" % half, offset=half * TABLE_BYTES + TABLE_BYTES // 2
-            )
-            nc.sync.dma_start(out=y_half[:], in_=y_tiles[:, half * TILES_PER_LOAD : (half + 1) * TILES_PER_LOAD, :])
             for jj in range(TILES_PER_LOAD):
                 x_raw.append(x_half[:, :, jj * P : (jj + 1) * P])
-                y_raw.append(y_half[:, jj, :])
+
+        def load_y(j):
+            place = TABLE_BYTES // 2 if j == 0 else 2 * TABLE_BYTES + j * 4 * SLOTS
+            y_tile = reuse.tile([P, SLOTS], F32, name="y_raw%d" % j, offset=place)
+            nc.sync.dma_start(out=y_tile[:], in_=y[0, j * P : (j + 1) * P, :])
+            y_raw.append(y_tile[:])
 
         ts_table = reuse.tile([P, ITEMS], F32, name="ts_table", offset=4 * TABLE_BYTES)
         ts_quarters = ts_table[:].rearrange("p (n q c) -> p q n c", q=PACK, c=PACK)
@@ -132,41 +132,64 @@ def tile_attend_gsq_x_ts_kernel(tc, xT, wT, y, wt, ts, offs, out):
             turn_banks.append(turn_bank)
 
         def copy_turned(t):
-            if t == PACK - 1:
-                turned = reuse.tile([P, P * PACK], BF16, name="w_by_slot%d" % t, align_bytes=64, offset=TABLE_BYTES // 2)
-            else:
-                turned = keep.tile([P, P * PACK], BF16, name="w_by_slot%d" % t, align_bytes=64)
+            if t == 0:
+                w_by_slot.append(keep.tile([P, 2 * P * PACK], BF16, name="w_by_slot0", align_bytes=64))
+            if t == 2:
+                w_by_slot.append(
+                    reuse.tile([P, 2 * P * PACK], BF16, name="w_by_slot1", align_bytes=64, offset=TABLE_BYTES // 2)
+                )
+            words = w_by_slot[t // 2][:].bitcast(F32).rearrange("s (h t p v) -> s t h p v", h=2, t=2, v=2)
             nc.scalar.copy(
-                out=turned[:].bitcast(F32).rearrange("s (p v) -> s p v", v=2),
-                in_=turn_banks[t][:].rearrange("s v p -> s p v"),
+                out=words[:, t % 2, :, :, :],
+                in_=turn_banks[t][:].rearrange("s v (h p) -> s h p v", h=2),
             )
-            w_by_slot.append(turned)
 
-        def quantise_turned(t):
-            cols = slice(t * P, (t + 1) * P)
-            nc.vector.quantize_mx(
-                out=wn_codes[:, cols].bitcast(E4M3),
-                scales=wn_scales[:, cols],
-                in_=w_by_slot[t][:],
-            )
+        def quantise_turned(pair):
+            for h in range(2):
+                cols = slice((2 * h + pair) * P, (2 * h + pair + 1) * P)
+                nc.vector.quantize_mx(
+                    out=wn_codes[:, cols].bitcast(E4M3),
+                    scales=wn_scales[:, cols],
+                    in_=w_by_slot[pair][:, h * P * PACK : (h + 1) * P * PACK],
+                )
 
         for t in range(PACK - 1):
             gather_plane(t)
             if t < 2:
-                load_rows(t)
+                load_x(t)
+            if t == 0:
+                load_y(0)
+            if t == 2:
+                for j in range(1, ROW_TILES):
+                    load_y(j)
             turn_plane(t)
-            copy_turned(t)
             if t < 2:
-                quantise_turned(t)
+                copy_turned(t)
             if t == 1:
+                quantise_turned(0)
                 woven, planes = weave_views(0)
                 nc.scalar.copy(out=woven, in_=planes)
-        gather_plane(PACK - 1)
+        last = PACK - 1
+        half = SLOTS // 2
+        nc.vector.tensor_copy(
+            out=pairs[1][:, SLOTS : SLOTS + half], in_=tables[last][:].indirect(offsets[:, 0 : half // 16])
+        )
+        nc.scalar.activation(
+            out=pairs[1][:, SLOTS + half : 2 * SLOTS],
+            in_=tables[last][:].indirect(offsets[:, half // 16 : SLOTS // 16]),
+            func=COPY,
+        )
         turn_plane(PACK - 1)
         woven, planes = weave_views(1)
-        nc.vector.tensor_copy(out=woven, in_=planes)
-        nc.vector.quantize_mx(out=wd_codes[:].bitcast(E4M3), scales=wd_scales, in_=w_by_d[:].rearrange("p c t -> p (c t)"))
-        quantise_turned(2)
+        for first in (0, half // 4):
+            nc.vector.tensor_copy(out=woven[:, first : first + half // 4], in_=planes[:, first : first + half // 4])
+
+        def quantise_woven(first):
+            nc.vector.quantize_mx(
+                out=wd_codes[:, first : first + half].bitcast(E4M3),
+                scales=wd_scales[:, first : first + half],
+                in_=w_by_d[:, first : first + half, :].rearrange("p c t -> p (c t)"),
+            )
 
         x_codes = []
         x_scales = []
@@ -176,31 +199,43 @@ def tile_attend_gsq_x_ts_kernel(tc, xT, wT, y, wt, ts, offs, out):
         score = {}
         h_in = {}
 
-        def prepare(j):
-            x_in = keep.tile([P, P, PACK], BF16, name="x_in%d" % j, align_bytes=64)
+        x_ins = []
+
+        def cast_x(j):
+            x_in = reuse.tile([P, P, PACK], BF16, name="x_in%d" % j, align_bytes=64, offset=5 * TABLE_BYTES + j * 4 * SLOTS)
             nc.scalar.copy(
                 out=x_in[:].rearrange("p (c i) t -> p c t i", i=4),
                 in_=x_raw[j].rearrange("p t (c i) -> p c t i", i=4),
             )
+            x_ins.append(x_in)
+
+        def quantise_x(j):
+            x_in = x_ins[j]
             codes = keep.tile([P, P], U32, name="x_codes%d" % j, tag="x_codes", bufs=2, align_bytes=64)
             scales = keep.tile([P, P], U8, name="x_scales%d" % j, align_bytes=64)
             nc.vector.quantize_mx(out=codes[:].bitcast(E4M3), scales=scales[:], in_=x_in[:].rearrange("p c t -> p (c t)"))
             x_codes.append(codes)
             x_scales.append(scales)
+
+        def multiply(j):
             bank = psum.tile([P, SLOTS], F32, name="score_bank%d" % j, tag="score")
-            nc.tensor.matmul_mx(
-                out=bank[:],
-                lhsT=codes[:].bitcast(E4M3),
-                lhsT_scale=scales[:],
-                rhs=wd_codes[:].bitcast(E4M3),
-                rhs_scale=wd_scales,
-                start=True,
-                stop=True,
-            )
+            width = half if j == 0 else SLOTS
+            for first in range(0, SLOTS, width):
+                cols = slice(first, first + width)
+                nc.tensor.matmul_mx(
+                    out=bank[:, cols],
+                    lhsT=x_codes[j][:].bitcast(E4M3),
+                    lhsT_scale=x_scales[j][:],
+                    rhs=wd_codes[:, cols].bitcast(E4M3),
+                    rhs_scale=wd_scales[:, cols],
+                    start=True,
+                    stop=True,
+                )
             score_bank.append(bank)
 
         def weigh_targets(j):
-            target = keep.tile([P, PACK, P], F32, name="y_neg%d" % j)
+            place = 5 * TABLE_BYTES + (1, 4, 5, 6)[j] * 4 * SLOTS
+            target = reuse.tile([P, PACK, P], F32, name="y_neg%d" % j, offset=place)
             nc.scalar.activation(
                 out=target[:].rearrange("r u s -> r s u"),
                 in_=y_raw[j].rearrange("r (s u) -> r s u", u=PACK),
@@ -221,12 +256,16 @@ def tile_attend_gsq_x_ts_kernel(tc, xT, wT, y, wt, ts, offs, out):
             )
             score[j] = scaled
 
-        def turn_gradient(j):
+        def turn_targets(j):
             bank = psum.tile([P, PACK, P], F32, name="grad_bank%d" % j, tag="grad" if j < 2 else "early")
+            grad_bank.append(bank)
             for u in range(PACK):
                 nc.tensor.matmul(
                     bank[:, u, :], lhsT=y_neg[j][:, u, :], rhs=ident_f32[:], start=(u == 0), stop=False, is_transpose=True
                 )
+
+        def turn_scores(j):
+            bank = grad_bank[j]
             for u in range(PACK):
                 nc.tensor.matmul(
                     bank[:, u, :],
@@ -236,7 +275,6 @@ def tile_attend_gsq_x_ts_kernel(tc, xT, wT, y, wt, ts, offs, out):
                     stop=(u == PACK - 1),
                     is_transpose=True,
                 )
-            grad_bank.append(bank)
 
         def scale_gradient(j):
             bank = grad_bank[j]
@@ -249,43 +287,81 @@ def tile_attend_gsq_x_ts_kernel(tc, xT, wT, y, wt, ts, offs, out):
             )
             h_in[j] = h_tile
 
-        def finish(j):
+        h_mx = {}
+
+        def quantise_h(j):
             codes = keep.tile([P, P], U32, name="h_codes%d" % j, align_bytes=64)
             scales = keep.tile([P, P], U8, name="h_scales%d" % j, align_bytes=64)
             nc.vector.quantize_mx(
                 out=codes[:].bitcast(E5M2), scales=scales[:], in_=h_in[j][:].rearrange("s r u -> s (r u)")
             )
-            bank = psum.tile([P, FEATURES], F32, name="out_bank%d" % j, tag="out")
+            h_mx[j] = (codes, scales)
+
+        def finish(j, first, width, tag, on_vector):
+            codes, scales = h_mx[j]
+            cols = slice(first, first + width)
+            bank = psum.tile([P, width], F32, name="out_bank%d_%d" % (j, first), tag=tag)
             nc.tensor.matmul_mx(
                 out=bank[:],
                 lhsT=codes[:].bitcast(E5M2),
                 lhsT_scale=scales[:],
-                rhs=wn_codes[:].bitcast(E4M3),
-                rhs_scale=wn_scales,
+                rhs=wn_codes[:, cols].bitcast(E4M3),
+                rhs_scale=wn_scales[:, cols],
                 start=True,
                 stop=True,
             )
-            result = keep.tile([P, P, PACK], F32, name="result%d" % j)
-            if j == ROW_TILES - 1:
-                nc.vector.tensor_copy(out=result[:], in_=bank[:].rearrange("r (t p) -> r p t", t=PACK))
+            result = keep.tile([P, width], F32, name="result%d_%d" % (j, first))
+            written = result[:].rearrange("r (h p t) -> r h p t", p=P // 2, t=PACK)
+            read = bank[:].rearrange("r (h t p) -> r h p t", p=P // 2, t=PACK)
+            if on_vector:
+                nc.vector.tensor_copy(out=written, in_=read)
             else:
-                nc.scalar.copy(out=result[:], in_=bank[:].rearrange("r (t p) -> r p t", t=PACK))
-            nc.sync.dma_start(out=out[0, j * P : (j + 1) * P, :], in_=result[:].rearrange("r p t -> r (p t)"))
+                nc.scalar.copy(out=written, in_=read)
+            nc.sync.dma_start(out=out[0, j * P : (j + 1) * P, cols], in_=result[:])
 
-        prepare(0)
-        prepare(1)
-        for step in range(ROW_TILES + 2):
-            if step < ROW_TILES:
-                scores(step)
-            if 2 <= step + 1 < ROW_TILES:
-                prepare(step + 1)
-            if step == 2:
-                copy_turned(PACK - 1)
-                quantise_turned(PACK - 1)
-            if step >= 2:
-                finish(step - 2)
-            if step < ROW_TILES:
-                weigh_targets(step)
-                turn_gradient(step)
-            if 1 <= step <= ROW_TILES:
-                scale_gradient(step - 1)
+        cast_x(0)
+        quantise_woven(0)
+        quantise_x(0)
+        quantise_woven(half)
+        multiply(0)
+        cast_x(1)
+        quantise_x(1)
+        multiply(1)
+        cast_x(2)
+        weigh_targets(0)
+        turn_targets(0)
+        scores(0)
+        cast_x(3)
+        copy_turned(2)
+        copy_turned(3)
+        scores(1)
+        turn_scores(0)
+        quantise_x(2)
+        multiply(2)
+        quantise_x(3)
+        multiply(3)
+        weigh_targets(1)
+        turn_targets(1)
+        turn_scores(1)
+        scale_gradient(0)
+        quantise_turned(1)
+        weigh_targets(2)
+        weigh_targets(3)
+        scores(2)
+        scale_gradient(1)
+        turn_targets(2)
+        turn_scores(2)
+        scores(3)
+        quantise_h(0)
+        finish(0, 0, FEATURES, "out", False)
+        turn_targets(3)
+        turn_scores(3)
+        quantise_h(1)
+        finish(1, 0, FEATURES, "out", False)
+        scale_gradient(2)
+        scale_gradient(3)
+        quantise_h(2)
+        finish(2, 0, FEATURES, "out", False)
+        quantise_h(3)
+        finish(3, 0, FEATURES // 2, "score", True)
+        finish(3, FEATURES // 2, FEATURES // 2, "score", False)

@@ -23,6 +23,9 @@ ROW_TILES = ROWS // P
 TILES_PER_LOAD = 2
 
 TABLE_BYTES = 4 * ITEMS
+Y0_OFFSET = 4 * TABLE_BYTES + 3 * 4 * SLOTS
+LISTED_OFFSET = 7 * TABLE_BYTES
+WOVEN_OFFSET = 8 * TABLE_BYTES
 
 FLOPS = 2 * 2 * ROWS * SLOTS * FEATURES
 
@@ -32,12 +35,12 @@ def tile_attend_gsq_x_ts_kernel(tc, xT, wT, y, wt, ts, offs, out):
     with ExitStack() as ctx:
         keep = ctx.enter_context(tc.tile_pool(name="keep", bufs=1))
         reuse = ctx.enter_context(tc.tile_pool(name="reuse", bufs=1))
-        psum = ctx.enter_context(tc.psum_pool(name="psum", bufs=2))
+        psum = ctx.enter_context(tc.psum_pool(name="psum", bufs=1))
 
         offsets = keep.tile([P, SLOTS // 16], U16, name="offsets")
         nc.sync.dma_start(offsets[:], offs)
 
-        ts_folded = reuse.tile([P, ITEMS // P], F32, name="ts_folded", offset=3 * TABLE_BYTES)
+        ts_folded = reuse.tile([P, ITEMS // P], F32, name="ts_folded", offset=WOVEN_OFFSET)
         nc.scalar.dma_start(out=ts_folded[:], in_=ts[0].rearrange("(n c) -> n c", n=P))
         wt_rows = keep.tile([P, P], F32, name="wt_rows")
         nc.gpsimd.memset(wt_rows[:], 0.0)
@@ -49,7 +52,7 @@ def tile_attend_gsq_x_ts_kernel(tc, xT, wT, y, wt, ts, offs, out):
         tables = []
         for t in range(PACK):
             tables.append(reuse.tile([P, ITEMS], F32, name="table%d" % t, offset=t * TABLE_BYTES))
-        for t in range(PACK - 1):
+        for t in range(PACK):
             nc.sync.dma_start(out=tables[t][:], in_=w_planes[:, t, :])
             if t == 0:
                 nc.sync.dma_start(out=wt_rows[0:ROW_TILES, :], in_=wt[0].rearrange("(j p) o -> j (p o)", p=P))
@@ -60,27 +63,27 @@ def tile_attend_gsq_x_ts_kernel(tc, xT, wT, y, wt, ts, offs, out):
 
         def load_x(half):
             width = TILES_PER_LOAD * P
-            x_half = reuse.tile([P, PACK, width], F32, name="x_raw%d" % half, offset=half * TABLE_BYTES)
+            place = (4 * TABLE_BYTES, LISTED_OFFSET)[half]
+            x_half = reuse.tile([P, PACK, width], F32, name="x_raw%d" % half, offset=place)
             nc.sync.dma_start(out=x_half[:], in_=x_planes[:, :, half * width : (half + 1) * width])
             for jj in range(TILES_PER_LOAD):
                 x_raw.append(x_half[:, :, jj * P : (jj + 1) * P])
 
         def load_y(j):
-            place = TABLE_BYTES // 2 if j == 0 else 2 * TABLE_BYTES + j * 4 * SLOTS
+            place = Y0_OFFSET if j == 0 else 2 * TABLE_BYTES + j * 4 * SLOTS
             y_tile = reuse.tile([P, SLOTS], F32, name="y_raw%d" % j, offset=place)
             nc.sync.dma_start(out=y_tile[:], in_=y[0, j * P : (j + 1) * P, :])
             y_raw.append(y_tile[:])
 
         ts_table = reuse.tile([P, ITEMS], F32, name="ts_table", offset=4 * TABLE_BYTES)
         ts_quarters = ts_table[:].rearrange("p (n q c) -> p q n c", q=PACK, c=PACK)
-        for q, tag in enumerate(("early", "score", "grad", "out")):
-            spread_bank = psum.tile([P, PACK, P], F32, name="spread_bank%d" % q, tag=tag)
+        for q in range(PACK):
+            spread_bank = psum.tile([P, PACK, P], F32, name="spread_bank%d" % q, tag="bank%d" % q)
             for c in range(PACK):
                 col = PACK * q + c
                 nc.tensor.transpose(spread_bank[:, c, :], ts_folded[:, col : col + 1].to_broadcast([P, P]), ident_f32[:])
             nc.scalar.activation(out=ts_quarters[:, q, :, :], in_=spread_bank[:].rearrange("p c n -> p n c"), func=COPY)
-        nc.sync.dma_start(out=tables[PACK - 1][:], in_=w_planes[:, PACK - 1, :])
-        ts_row = keep.tile([P, SLOTS], F32, name="ts_row")
+        ts_row = reuse.tile([P, SLOTS], F32, name="ts_row", offset=LISTED_OFFSET)
         nc.vector.tensor_copy(out=ts_row[:], in_=ts_table[:].indirect(offsets[:]))
         ts_spread = keep.tile([P, SLOTS], F32, name="ts_spread")
         nc.scalar.activation(
@@ -89,24 +92,24 @@ def tile_attend_gsq_x_ts_kernel(tc, xT, wT, y, wt, ts, offs, out):
             func=COPY,
             scale=-1.0,
         )
-        ts_bank = psum.tile([P, PACK, P], F32, name="ts_bank", tag="grad")
+        ts_bank = psum.tile([P, PACK, P], F32, name="ts_bank", tag="bank4")
         for u in range(PACK):
             nc.tensor.transpose(ts_bank[:, u, :], ts_spread[:, u * P : (u + 1) * P], ident_f32[:])
         ts_cols = keep.tile([P, PACK], F32, name="ts_cols")
         nc.scalar.copy(out=ts_cols[:], in_=ts_bank[:, :, 0])
 
-        wt_bank = psum.tile([P, P], F32, name="wt_bank", tag="out")
+        wt_bank = psum.tile([P, P], F32, name="wt_bank", tag="bank5")
         nc.tensor.transpose(wt_bank[:], wt_rows[:], ident_f32[:])
         wt_cols = keep.tile([P, ROW_TILES], F32, name="wt_cols")
         nc.scalar.copy(out=wt_cols[:], in_=wt_bank[:, 0:ROW_TILES])
 
-        w_by_d = keep.tile([P, SLOTS, PACK], BF16, name="w_by_d", align_bytes=64)
+        w_by_d = reuse.tile([P, SLOTS, PACK], BF16, name="w_by_d", align_bytes=64, offset=WOVEN_OFFSET)
         pairs = [
-            reuse.tile([P, 2 * SLOTS], BF16, name="pair0", offset=4 * TABLE_BYTES),
+            keep.tile([P, 2 * SLOTS], BF16, name="pair0"),
             reuse.tile([P, 2 * SLOTS], BF16, name="pair1", offset=4 * TABLE_BYTES + TABLE_BYTES // 2),
         ]
         wn_codes = keep.tile([P, FEATURES], U32, name="wn_codes", align_bytes=64)
-        w_scales = keep.tile([P, SLOTS], U8, name="w_scales", align_bytes=64)
+        w_scales = reuse.tile([P, SLOTS], U8, name="w_scales", align_bytes=64, offset=2 * TABLE_BYTES)
         wn_scales = w_scales[:]
         wd_scales = w_scales[4:P, :]
         wd_codes = keep.tile([P, SLOTS], U32, name="wd_codes", align_bytes=64)
@@ -126,7 +129,7 @@ def tile_attend_gsq_x_ts_kernel(tc, xT, wT, y, wt, ts, offs, out):
         def turn_plane(t):
             words = pairs[t // 2][:].bitcast(F32)
             first = (t % 2) * (SLOTS // 2)
-            turn_bank = psum.tile([P, 2, P], F32, name="turn_bank%d" % t, tag="early")
+            turn_bank = psum.tile([P, 2, P], F32, name="turn_bank%d" % t, tag="bank%d" % (3 - t % 2))
             for v in range(2):
                 nc.tensor.transpose(turn_bank[:, v, :], words[:, first + v : first + SLOTS // 2 : 2], ident_f32[:])
             turn_banks.append(turn_bank)
@@ -136,7 +139,7 @@ def tile_attend_gsq_x_ts_kernel(tc, xT, wT, y, wt, ts, offs, out):
                 w_by_slot.append(keep.tile([P, 2 * P * PACK], BF16, name="w_by_slot0", align_bytes=64))
             if t == 2:
                 w_by_slot.append(
-                    reuse.tile([P, 2 * P * PACK], BF16, name="w_by_slot1", align_bytes=64, offset=TABLE_BYTES // 2)
+                    reuse.tile([P, 2 * P * PACK], BF16, name="w_by_slot1", align_bytes=64, offset=Y0_OFFSET)
                 )
             words = w_by_slot[t // 2][:].bitcast(F32).rearrange("s (h t p v) -> s t h p v", h=2, t=2, v=2)
             nc.scalar.copy(
@@ -218,7 +221,7 @@ def tile_attend_gsq_x_ts_kernel(tc, xT, wT, y, wt, ts, offs, out):
             x_scales.append(scales)
 
         def multiply(j):
-            bank = psum.tile([P, SLOTS], F32, name="score_bank%d" % j, tag="score")
+            bank = psum.tile([P, SLOTS], F32, name="score_bank%d" % j, tag="bank%d" % (j % 2))
             width = half if j == 0 else SLOTS
             for first in range(0, SLOTS, width):
                 cols = slice(first, first + width)
@@ -257,7 +260,7 @@ def tile_attend_gsq_x_ts_kernel(tc, xT, wT, y, wt, ts, offs, out):
             score[j] = scaled
 
         def turn_targets(j):
-            bank = psum.tile([P, PACK, P], F32, name="grad_bank%d" % j, tag="grad" if j < 2 else "early")
+            bank = psum.tile([P, PACK, P], F32, name="grad_bank%d" % j, tag="bank%d" % (4, 5, 2, 3)[j])
             grad_bank.append(bank)
             for u in range(PACK):
                 nc.tensor.matmul(
@@ -300,7 +303,7 @@ def tile_attend_gsq_x_ts_kernel(tc, xT, wT, y, wt, ts, offs, out):
         def finish(j, first, width, tag, on_vector):
             codes, scales = h_mx[j]
             cols = slice(first, first + width)
-            bank = psum.tile([P, width], F32, name="out_bank%d_%d" % (j, first), tag=tag)
+            bank = psum.tile([P, width], F32, name="out_bank%d_%d" % (j, first), tag="bank%d" % tag)
             nc.tensor.matmul_mx(
                 out=bank[:],
                 lhsT=codes[:].bitcast(E5M2),
@@ -353,15 +356,15 @@ def tile_attend_gsq_x_ts_kernel(tc, xT, wT, y, wt, ts, offs, out):
         turn_scores(2)
         scores(3)
         quantise_h(0)
-        finish(0, 0, FEATURES, "out", False)
+        finish(0, 0, FEATURES, 6, False)
         turn_targets(3)
         turn_scores(3)
         quantise_h(1)
-        finish(1, 0, FEATURES, "out", False)
+        finish(1, 0, FEATURES, 7, False)
         scale_gradient(2)
         scale_gradient(3)
         quantise_h(2)
-        finish(2, 0, FEATURES, "out", False)
+        finish(2, 0, FEATURES, 6, False)
         quantise_h(3)
-        finish(3, 0, FEATURES // 2, "score", True)
-        finish(3, FEATURES // 2, FEATURES // 2, "score", False)
+        finish(3, 0, FEATURES // 2, 0, True)
+        finish(3, FEATURES // 2, FEATURES // 2, 1, False)

@@ -23,8 +23,7 @@ ROW_TILES = ROWS // P
 TILES_PER_LOAD = 2
 
 TABLE_BYTES = 4 * ITEMS
-Y0_OFFSET = 4 * TABLE_BYTES + 3 * 4 * SLOTS
-LISTED_OFFSET = 7 * TABLE_BYTES
+Y0_OFFSET = 7 * TABLE_BYTES
 WOVEN_OFFSET = 8 * TABLE_BYTES
 
 FLOPS = 2 * 2 * ROWS * SLOTS * FEATURES
@@ -40,9 +39,9 @@ def tile_attend_gsq_x_ts_kernel(tc, xT, wT, y, wt, ts, offs, out):
         offsets = keep.tile([P, SLOTS // 16], U16, name="offsets")
         nc.sync.dma_start(offsets[:], offs)
 
-        ts_folded = reuse.tile([P, ITEMS // P], F32, name="ts_folded", offset=WOVEN_OFFSET)
+        ts_folded = reuse.tile([P, ITEMS // P], F32, name="ts_folded", offset=WOVEN_OFFSET - 32)
         nc.scalar.dma_start(out=ts_folded[:], in_=ts[0].rearrange("(n c) -> n c", n=P))
-        wt_rows = keep.tile([P, P], F32, name="wt_rows")
+        wt_rows = reuse.tile([P, P], F32, name="wt_rows", offset=Y0_OFFSET)
         nc.gpsimd.memset(wt_rows[:], 0.0)
 
         ident_f32 = keep.tile([P, P], F32, name="ident_f32")
@@ -63,7 +62,7 @@ def tile_attend_gsq_x_ts_kernel(tc, xT, wT, y, wt, ts, offs, out):
 
         def load_x(half):
             width = TILES_PER_LOAD * P
-            place = (4 * TABLE_BYTES, LISTED_OFFSET)[half]
+            place = (WOVEN_OFFSET - TABLE_BYTES // 2, 4 * TABLE_BYTES)[half]
             x_half = reuse.tile([P, PACK, width], F32, name="x_raw%d" % half, offset=place)
             nc.sync.dma_start(out=x_half[:], in_=x_planes[:, :, half * width : (half + 1) * width])
             for jj in range(TILES_PER_LOAD):
@@ -83,7 +82,7 @@ def tile_attend_gsq_x_ts_kernel(tc, xT, wT, y, wt, ts, offs, out):
                 col = PACK * q + c
                 nc.tensor.transpose(spread_bank[:, c, :], ts_folded[:, col : col + 1].to_broadcast([P, P]), ident_f32[:])
             nc.scalar.activation(out=ts_quarters[:, q, :, :], in_=spread_bank[:].rearrange("p c n -> p n c"), func=COPY)
-        ts_row = reuse.tile([P, SLOTS], F32, name="ts_row", offset=LISTED_OFFSET)
+        ts_row = keep.tile([P, SLOTS], F32, name="ts_row")
         nc.vector.tensor_copy(out=ts_row[:], in_=ts_table[:].indirect(offsets[:]))
         ts_spread = keep.tile([P, SLOTS], F32, name="ts_spread")
         nc.scalar.activation(

@@ -21,10 +21,12 @@ FEATURES = 512
 ROWS = 512
 ROW_TILES = ROWS // P
 TILES_PER_LOAD = 2
+ZEROED_BY_VECTOR = 1536
 
 TABLE_BYTES = 4 * ITEMS
 Y0_OFFSET = 7 * TABLE_BYTES
 WOVEN_OFFSET = 8 * TABLE_BYTES
+CAST_OFFSET = 9 * TABLE_BYTES
 
 FLOPS = 2 * 2 * ROWS * SLOTS * FEATURES
 
@@ -36,17 +38,15 @@ def tile_attend_gsq_x_ts_kernel(tc, xT, wT, y, wt, ts, offs, out):
         reuse = ctx.enter_context(tc.tile_pool(name="reuse", bufs=1))
         psum = ctx.enter_context(tc.psum_pool(name="psum", bufs=1))
 
-        offsets = keep.tile([P, SLOTS // 16], U16, name="offsets")
-        nc.sync.dma_start(offsets[:], offs)
-
-        ts_folded = reuse.tile([P, ITEMS // P], F32, name="ts_folded", offset=WOVEN_OFFSET - 32)
-        nc.scalar.dma_start(out=ts_folded[:], in_=ts[0].rearrange("(n c) -> n c", n=P))
         wt_rows = reuse.tile([P, P], F32, name="wt_rows", offset=Y0_OFFSET)
         nc.gpsimd.memset(wt_rows[:], 0.0)
-
+        ts_table = reuse.tile([P, ITEMS], F32, name="ts_table", offset=4 * TABLE_BYTES)
+        nc.vector.memset(ts_table[:, 0:ZEROED_BY_VECTOR].bitcast(U32), 0)
+        nc.gpsimd.memset(ts_table[:, ZEROED_BY_VECTOR:ITEMS], 0.0)
         ident_f32 = keep.tile([P, P], F32, name="ident_f32")
         make_identity(nc, ident_f32[:])
 
+        offsets = keep.tile([P, SLOTS // 16], U16, name="offsets")
         w_planes = wT.rearrange("(p t) c -> p t c", t=PACK)
         tables = []
         for t in range(PACK):
@@ -54,7 +54,9 @@ def tile_attend_gsq_x_ts_kernel(tc, xT, wT, y, wt, ts, offs, out):
         for t in range(PACK):
             nc.sync.dma_start(out=tables[t][:], in_=w_planes[:, t, :])
             if t == 0:
+                nc.sync.dma_start(offsets[:], offs)
                 nc.sync.dma_start(out=wt_rows[0:ROW_TILES, :], in_=wt[0].rearrange("(j p) o -> j (p o)", p=P))
+                nc.sync.dma_start(out=ts_table[0:1, :], in_=ts[0:1, :])
 
         x_planes = xT[0].rearrange("(p t) r -> p t r", t=PACK)
         x_raw = []
@@ -69,33 +71,32 @@ def tile_attend_gsq_x_ts_kernel(tc, xT, wT, y, wt, ts, offs, out):
                 x_raw.append(x_half[:, :, jj * P : (jj + 1) * P])
 
         def load_y(j):
-            place = Y0_OFFSET if j == 0 else 2 * TABLE_BYTES + j * 4 * SLOTS
+            place = 5 * TABLE_BYTES - 4 * SLOTS if j == 0 else 2 * TABLE_BYTES + j * 4 * SLOTS
             y_tile = reuse.tile([P, SLOTS], F32, name="y_raw%d" % j, offset=place)
             nc.sync.dma_start(out=y_tile[:], in_=y[0, j * P : (j + 1) * P, :])
             y_raw.append(y_tile[:])
 
-        ts_table = reuse.tile([P, ITEMS], F32, name="ts_table", offset=4 * TABLE_BYTES)
-        ts_quarters = ts_table[:].rearrange("p (n q c) -> p q n c", q=PACK, c=PACK)
-        for q in range(PACK):
-            spread_bank = psum.tile([P, PACK, P], F32, name="spread_bank%d" % q, tag="bank%d" % q)
-            for c in range(PACK):
-                col = PACK * q + c
-                nc.tensor.transpose(spread_bank[:, c, :], ts_folded[:, col : col + 1].to_broadcast([P, P]), ident_f32[:])
-            nc.scalar.activation(out=ts_quarters[:, q, :, :], in_=spread_bank[:].rearrange("p c n -> p n c"), func=COPY)
         ts_row = keep.tile([P, SLOTS], F32, name="ts_row")
         nc.vector.tensor_copy(out=ts_row[:], in_=ts_table[:].indirect(offsets[:]))
-        ts_spread = keep.tile([P, SLOTS], F32, name="ts_spread")
+        ts_dealt = keep.tile([P, SLOTS], F32, name="ts_dealt")
         nc.scalar.activation(
-            out=ts_spread[:].rearrange("p (u s) -> p s u", u=PACK),
+            out=ts_dealt[:].rearrange("p (u s) -> p s u", u=PACK),
             in_=ts_row[:].rearrange("p (s u) -> p s u", u=PACK),
             func=COPY,
             scale=-1.0,
         )
         ts_bank = psum.tile([P, PACK, P], F32, name="ts_bank", tag="bank4")
         for u in range(PACK):
-            nc.tensor.transpose(ts_bank[:, u, :], ts_spread[:, u * P : (u + 1) * P], ident_f32[:])
+            nc.tensor.transpose(ts_bank[:, u, :], ts_dealt[:, u * P : (u + 1) * P], ident_f32[:])
+        ts_wide = keep.tile([P, PACK, P], F32, name="ts_wide")
+        nc.scalar.copy(out=ts_wide[:], in_=ts_bank[:, :, 0:1].to_broadcast([P, PACK, P]))
         ts_cols = keep.tile([P, PACK], F32, name="ts_cols")
         nc.scalar.copy(out=ts_cols[:], in_=ts_bank[:, :, 0])
+        spread_bank = psum.tile([P, PACK, P], F32, name="spread_bank", tag="bank6")
+        for u in range(PACK):
+            nc.tensor.transpose(spread_bank[:, u, :], ts_wide[:, u, :], ident_f32[:])
+        ts_spread = keep.tile([P, SLOTS], F32, name="ts_spread")
+        nc.scalar.copy(out=ts_spread[:], in_=spread_bank[:].rearrange("p u s -> p (u s)"))
 
         wt_bank = psum.tile([P, P], F32, name="wt_bank", tag="bank5")
         nc.tensor.transpose(wt_bank[:], wt_rows[:], ident_f32[:])
@@ -128,7 +129,7 @@ def tile_attend_gsq_x_ts_kernel(tc, xT, wT, y, wt, ts, offs, out):
         def turn_plane(t):
             words = pairs[t // 2][:].bitcast(F32)
             first = (t % 2) * (SLOTS // 2)
-            turn_bank = psum.tile([P, 2, P], F32, name="turn_bank%d" % t, tag="bank%d" % (3 - t % 2))
+            turn_bank = psum.tile([P, 2, P], F32, name="turn_bank%d" % t, tag="bank%d" % (3, 2, 6, 2)[t])
             for v in range(2):
                 nc.tensor.transpose(turn_bank[:, v, :], words[:, first + v : first + SLOTS // 2 : 2], ident_f32[:])
             turn_banks.append(turn_bank)
@@ -138,7 +139,7 @@ def tile_attend_gsq_x_ts_kernel(tc, xT, wT, y, wt, ts, offs, out):
                 w_by_slot.append(keep.tile([P, 2 * P * PACK], BF16, name="w_by_slot0", align_bytes=64))
             if t == 2:
                 w_by_slot.append(
-                    reuse.tile([P, 2 * P * PACK], BF16, name="w_by_slot1", align_bytes=64, offset=Y0_OFFSET)
+                    reuse.tile([P, 2 * P * PACK], BF16, name="w_by_slot1", align_bytes=64, offset=4 * TABLE_BYTES)
                 )
             words = w_by_slot[t // 2][:].bitcast(F32).rearrange("s (h t p v) -> s t h p v", h=2, t=2, v=2)
             nc.scalar.copy(
@@ -159,7 +160,7 @@ def tile_attend_gsq_x_ts_kernel(tc, xT, wT, y, wt, ts, offs, out):
             gather_plane(t)
             if t < 2:
                 load_x(t)
-            if t == 0:
+            if t == 1:
                 load_y(0)
             if t == 2:
                 for j in range(1, ROW_TILES):
@@ -168,9 +169,9 @@ def tile_attend_gsq_x_ts_kernel(tc, xT, wT, y, wt, ts, offs, out):
             if t < 2:
                 copy_turned(t)
             if t == 1:
-                quantise_turned(0)
                 woven, planes = weave_views(0)
-                nc.scalar.copy(out=woven, in_=planes)
+                nc.vector.tensor_copy(out=woven, in_=planes)
+                quantise_turned(0)
         last = PACK - 1
         half = SLOTS // 2
         nc.vector.tensor_copy(
@@ -204,39 +205,52 @@ def tile_attend_gsq_x_ts_kernel(tc, xT, wT, y, wt, ts, offs, out):
         x_ins = []
 
         def cast_x(j):
-            x_in = reuse.tile([P, P, PACK], BF16, name="x_in%d" % j, align_bytes=64, offset=5 * TABLE_BYTES + j * 4 * SLOTS)
-            nc.scalar.copy(
-                out=x_in[:].rearrange("p (c i) t -> p c t i", i=4),
+            if j < 3:
+                count = 1 if j < 2 else 2
+                x_ins.append(
+                    reuse.tile(
+                        [P, count * P, PACK], BF16, name="x_in%d" % j, align_bytes=64, offset=CAST_OFFSET + j * TABLE_BYTES
+                    )
+                )
+            x_in = x_ins[min(j, 2)][:, (j // 3) * P : (j // 3 + 1) * P, :]
+            copy = nc.vector.tensor_copy if j == 3 else nc.scalar.copy
+            copy(
+                out=x_in.rearrange("p (c i) t -> p c t i", i=4),
                 in_=x_raw[j].rearrange("p t (c i) -> p c t i", i=4),
             )
-            x_ins.append(x_in)
 
         def quantise_x(j):
-            x_in = x_ins[j]
-            codes = keep.tile([P, P], U32, name="x_codes%d" % j, tag="x_codes", bufs=2, align_bytes=64)
-            scales = keep.tile([P, P], U8, name="x_scales%d" % j, align_bytes=64)
-            nc.vector.quantize_mx(out=codes[:].bitcast(E4M3), scales=scales[:], in_=x_in[:].rearrange("p c t -> p (c t)"))
-            x_codes.append(codes)
-            x_scales.append(scales)
+            count = 1 if j < 2 else 2
+            codes = keep.tile([P, count * P], U32, name="x_codes%d" % j, align_bytes=64)
+            scales = keep.tile([P, count * P], U8, name="x_scales%d" % j, align_bytes=64)
+            nc.vector.quantize_mx(
+                out=codes[:].bitcast(E4M3), scales=scales[:], in_=x_ins[j][:].rearrange("p c t -> p (c t)")
+            )
+            for n in range(count):
+                x_codes.append(codes[:, n * P : (n + 1) * P])
+                x_scales.append(scales[:, n * P : (n + 1) * P])
 
         def multiply(j):
-            bank = psum.tile([P, SLOTS], F32, name="score_bank%d" % j, tag="bank%d" % (j % 2))
-            width = half if j == 0 else SLOTS
+            width = SLOTS
+            banks = []
             for first in range(0, SLOTS, width):
                 cols = slice(first, first + width)
+                tag = "bank%d" % ((0, 3, 7, 5)[j] + first // half)
+                bank = psum.tile([P, width], F32, name="score_bank%d_%d" % (j, first), tag=tag)
                 nc.tensor.matmul_mx(
-                    out=bank[:, cols],
-                    lhsT=x_codes[j][:].bitcast(E4M3),
-                    lhsT_scale=x_scales[j][:],
+                    out=bank[:],
+                    lhsT=x_codes[j].bitcast(E4M3),
+                    lhsT_scale=x_scales[j],
                     rhs=wd_codes[:, cols].bitcast(E4M3),
                     rhs_scale=wd_scales[:, cols],
                     start=True,
                     stop=True,
                 )
-            score_bank.append(bank)
+                banks.append(bank)
+            score_bank.append(banks)
 
         def weigh_targets(j):
-            place = 5 * TABLE_BYTES + (1, 4, 5, 6)[j] * 4 * SLOTS
+            place = CAST_OFFSET + 2 * TABLE_BYTES - 4 * SLOTS + 64 if j == 0 else 5 * TABLE_BYTES + j * 4 * SLOTS
             target = reuse.tile([P, PACK, P], F32, name="y_neg%d" % j, offset=place)
             nc.scalar.activation(
                 out=target[:].rearrange("r u s -> r s u"),
@@ -247,19 +261,28 @@ def tile_attend_gsq_x_ts_kernel(tc, xT, wT, y, wt, ts, offs, out):
             y_neg.append(target)
 
         def scores(j):
-            scaled = keep.tile([P, PACK, P], F32, name="score%d" % j)
-            nc.vector.scalar_tensor_tensor(
-                out=scaled[:],
-                in0=score_bank[j][:].rearrange("r (s u) -> r u s", u=PACK),
-                scalar=wt_cols[:, j : j + 1],
-                in1=ts_spread[:].rearrange("p (u s) -> p u s", u=PACK),
-                op0=MULT,
-                op1=MULT,
-            )
+            if j == 0:
+                place = CAST_OFFSET + 2 * TABLE_BYTES + 4 * SLOTS - 64
+                score["pair"] = reuse.tile([P, 2, PACK, P], F32, name="score_pair", offset=place)
+            if j < 2:
+                scaled = score["pair"][:, j]
+            else:
+                scaled = keep.tile([P, PACK, P], F32, name="score%d" % j)
+            words = P // len(score_bank[j])
+            for n, bank in enumerate(score_bank[j]):
+                part = slice(n * words, (n + 1) * words)
+                nc.vector.scalar_tensor_tensor(
+                    out=scaled[:, :, part],
+                    in0=bank[:].rearrange("r (s u) -> r u s", u=PACK),
+                    scalar=wt_cols[:, j : j + 1],
+                    in1=ts_spread[:].rearrange("p (u s) -> p u s", u=PACK)[:, :, part],
+                    op0=MULT,
+                    op1=MULT,
+                )
             score[j] = scaled
 
         def turn_targets(j):
-            bank = psum.tile([P, PACK, P], F32, name="grad_bank%d" % j, tag="bank%d" % (4, 5, 2, 3)[j])
+            bank = psum.tile([P, PACK, P], F32, name="grad_bank%d" % j, tag="bank%d" % (4, 0, 2, 6)[j])
             grad_bank.append(bank)
             for u in range(PACK):
                 nc.tensor.matmul(
@@ -290,6 +313,7 @@ def tile_attend_gsq_x_ts_kernel(tc, xT, wT, y, wt, ts, offs, out):
             h_in[j] = h_tile
 
         h_mx = {}
+        results = []
 
         def quantise_h(j):
             codes = keep.tile([P, P], U32, name="h_codes%d" % j, align_bytes=64)
@@ -319,7 +343,9 @@ def tile_attend_gsq_x_ts_kernel(tc, xT, wT, y, wt, ts, offs, out):
                 nc.vector.tensor_copy(out=written, in_=read)
             else:
                 nc.scalar.copy(out=written, in_=read)
-            nc.sync.dma_start(out=out[0, j * P : (j + 1) * P, cols], in_=result[:])
+            queue = nc.scalar if first > 0 else nc.sync
+            queue.dma_start(out=out[0, j * P : (j + 1) * P, cols], in_=result[:])
+            results.append(result)
 
         cast_x(0)
         quantise_woven(0)
@@ -330,40 +356,39 @@ def tile_attend_gsq_x_ts_kernel(tc, xT, wT, y, wt, ts, offs, out):
         quantise_x(1)
         multiply(1)
         cast_x(2)
-        weigh_targets(0)
-        turn_targets(0)
-        scores(0)
         cast_x(3)
+        quantise_x(2)
+        scores(0)
+        multiply(2)
+        multiply(3)
         copy_turned(2)
         copy_turned(3)
+        weigh_targets(0)
         scores(1)
+        turn_targets(0)
         turn_scores(0)
-        quantise_x(2)
-        multiply(2)
-        quantise_x(3)
-        multiply(3)
+        scores(2)
         weigh_targets(1)
         turn_targets(1)
         turn_scores(1)
         scale_gradient(0)
+        scores(3)
         quantise_turned(1)
         weigh_targets(2)
         weigh_targets(3)
-        scores(2)
-        scale_gradient(1)
         turn_targets(2)
         turn_scores(2)
-        scores(3)
         quantise_h(0)
-        finish(0, 0, FEATURES, 6, False)
+        finish(0, 0, FEATURES, 1, False)
+        scale_gradient(1)
         turn_targets(3)
         turn_scores(3)
         quantise_h(1)
-        finish(1, 0, FEATURES, 7, False)
+        finish(1, 0, FEATURES, 3, False)
         scale_gradient(2)
         scale_gradient(3)
         quantise_h(2)
-        finish(2, 0, FEATURES, 6, False)
+        finish(2, 0, FEATURES, 7, False)
         quantise_h(3)
-        finish(3, 0, FEATURES // 2, 0, True)
+        finish(3, 0, FEATURES // 2, 5, True)
         finish(3, FEATURES // 2, FEATURES // 2, 1, False)

@@ -22,11 +22,15 @@ ROWS = 512
 ROW_TILES = ROWS // P
 TILES_PER_LOAD = 2
 ZEROED_BY_VECTOR = 1536
+TS_ROW = P - 1
+WT_ROW = 60
 
 TABLE_BYTES = 4 * ITEMS
 Y0_OFFSET = 7 * TABLE_BYTES
 WOVEN_OFFSET = 8 * TABLE_BYTES
 CAST_OFFSET = 9 * TABLE_BYTES
+TURNED_OFFSET = 12 * TABLE_BYTES
+SCORE_OFFSET = 13 * TABLE_BYTES
 
 FLOPS = 2 * 2 * ROWS * SLOTS * FEATURES
 
@@ -39,10 +43,11 @@ def tile_attend_gsq_x_ts_kernel(tc, xT, wT, y, wt, ts, offs, out):
         psum = ctx.enter_context(tc.psum_pool(name="psum", bufs=1))
 
         wt_rows = reuse.tile([P, P], F32, name="wt_rows", offset=Y0_OFFSET)
-        nc.gpsimd.memset(wt_rows[:], 0.0)
+        nc.gpsimd.memset(wt_rows[0:WT_ROW, :], 0.0)
+        nc.gpsimd.memset(wt_rows[WT_ROW + ROW_TILES : P, :], 0.0)
         ts_table = reuse.tile([P, ITEMS], F32, name="ts_table", offset=4 * TABLE_BYTES)
-        nc.vector.memset(ts_table[:, 0:ZEROED_BY_VECTOR].bitcast(U32), 0)
-        nc.gpsimd.memset(ts_table[:, ZEROED_BY_VECTOR:ITEMS], 0.0)
+        nc.vector.memset(ts_table[0:TS_ROW, 0:ZEROED_BY_VECTOR].bitcast(U32), 0)
+        nc.gpsimd.memset(ts_table[0:TS_ROW, ZEROED_BY_VECTOR:ITEMS], 0.0)
         ident_f32 = keep.tile([P, P], F32, name="ident_f32")
         make_identity(nc, ident_f32[:])
 
@@ -55,8 +60,10 @@ def tile_attend_gsq_x_ts_kernel(tc, xT, wT, y, wt, ts, offs, out):
             nc.sync.dma_start(out=tables[t][:], in_=w_planes[:, t, :])
             if t == 0:
                 nc.sync.dma_start(offsets[:], offs)
-                nc.sync.dma_start(out=wt_rows[0:ROW_TILES, :], in_=wt[0].rearrange("(j p) o -> j (p o)", p=P))
-                nc.sync.dma_start(out=ts_table[0:1, :], in_=ts[0:1, :])
+                nc.scalar.dma_start(out=ts_table[TS_ROW : TS_ROW + 1, :], in_=ts[0:1, :])
+                nc.scalar.dma_start(
+                    out=wt_rows[WT_ROW : WT_ROW + ROW_TILES, :], in_=wt[0].rearrange("(j p) o -> j (p o)", p=P)
+                )
 
         x_planes = xT[0].rearrange("(p t) r -> p t r", t=PACK)
         x_raw = []
@@ -89,9 +96,9 @@ def tile_attend_gsq_x_ts_kernel(tc, xT, wT, y, wt, ts, offs, out):
         for u in range(PACK):
             nc.tensor.transpose(ts_bank[:, u, :], ts_dealt[:, u * P : (u + 1) * P], ident_f32[:])
         ts_wide = keep.tile([P, PACK, P], F32, name="ts_wide")
-        nc.scalar.copy(out=ts_wide[:], in_=ts_bank[:, :, 0:1].to_broadcast([P, PACK, P]))
+        nc.scalar.copy(out=ts_wide[:], in_=ts_bank[:, :, TS_ROW : TS_ROW + 1].to_broadcast([P, PACK, P]))
         ts_cols = keep.tile([P, PACK], F32, name="ts_cols")
-        nc.scalar.copy(out=ts_cols[:], in_=ts_bank[:, :, 0])
+        nc.scalar.copy(out=ts_cols[:], in_=ts_bank[:, :, TS_ROW])
         spread_bank = psum.tile([P, PACK, P], F32, name="spread_bank", tag="bank6")
         for u in range(PACK):
             nc.tensor.transpose(spread_bank[:, u, :], ts_wide[:, u, :], ident_f32[:])
@@ -101,7 +108,7 @@ def tile_attend_gsq_x_ts_kernel(tc, xT, wT, y, wt, ts, offs, out):
         wt_bank = psum.tile([P, P], F32, name="wt_bank", tag="bank5")
         nc.tensor.transpose(wt_bank[:], wt_rows[:], ident_f32[:])
         wt_cols = keep.tile([P, ROW_TILES], F32, name="wt_cols")
-        nc.scalar.copy(out=wt_cols[:], in_=wt_bank[:, 0:ROW_TILES])
+        nc.scalar.copy(out=wt_cols[:], in_=wt_bank[:, WT_ROW : WT_ROW + ROW_TILES])
 
         w_by_d = reuse.tile([P, SLOTS, PACK], BF16, name="w_by_d", align_bytes=64, offset=WOVEN_OFFSET)
         pairs = [
@@ -111,7 +118,6 @@ def tile_attend_gsq_x_ts_kernel(tc, xT, wT, y, wt, ts, offs, out):
         wn_codes = keep.tile([P, FEATURES], U32, name="wn_codes", align_bytes=64)
         w_scales = reuse.tile([P, SLOTS], U8, name="w_scales", align_bytes=64, offset=2 * TABLE_BYTES)
         wn_scales = w_scales[:]
-        wd_scales = w_scales[4:P, :]
         wd_codes = keep.tile([P, SLOTS], U32, name="wd_codes", align_bytes=64)
         w_by_slot = []
 
@@ -136,24 +142,27 @@ def tile_attend_gsq_x_ts_kernel(tc, xT, wT, y, wt, ts, offs, out):
 
         def copy_turned(t):
             if t == 0:
-                w_by_slot.append(keep.tile([P, 2 * P * PACK], BF16, name="w_by_slot0", align_bytes=64))
-            if t == 2:
                 w_by_slot.append(
-                    reuse.tile([P, 2 * P * PACK], BF16, name="w_by_slot1", align_bytes=64, offset=4 * TABLE_BYTES)
+                    reuse.tile([P, 2 * P * PACK], BF16, name="w_by_slot0", align_bytes=64, offset=TURNED_OFFSET)
                 )
-            words = w_by_slot[t // 2][:].bitcast(F32).rearrange("s (h t p v) -> s t h p v", h=2, t=2, v=2)
-            nc.scalar.copy(
-                out=words[:, t % 2, :, :, :],
-                in_=turn_banks[t][:].rearrange("s v (h p) -> s h p v", h=2),
-            )
+            if t < 2:
+                words = w_by_slot[0][:].bitcast(F32).rearrange("s (h t p v) -> s t h p v", h=2, t=2, v=2)[:, t]
+            else:
+                place = (3 * TABLE_BYTES, 4 * TABLE_BYTES - 2 * SLOTS + 64)[t - 2]
+                w_by_slot.append(
+                    reuse.tile([P, P * PACK], BF16, name="w_by_slot%d" % t, align_bytes=64, offset=place)
+                )
+                words = w_by_slot[t - 1][:].bitcast(F32).rearrange("s (h p v) -> s h p v", h=2, v=2)
+            nc.scalar.copy(out=words, in_=turn_banks[t][:].rearrange("s v (h p) -> s h p v", h=2))
 
-        def quantise_turned(pair):
+        def quantise_turned(first, count):
+            width = count * P // 2
             for h in range(2):
-                cols = slice((2 * h + pair) * P, (2 * h + pair + 1) * P)
+                start = (PACK * h + first) * P // 2
                 nc.vector.quantize_mx(
-                    out=wn_codes[:, cols].bitcast(E4M3),
-                    scales=wn_scales[:, cols],
-                    in_=w_by_slot[pair][:, h * P * PACK : (h + 1) * P * PACK],
+                    out=wn_codes[:, start : start + width].bitcast(E4M3),
+                    scales=wn_scales[:, start : start + width],
+                    in_=w_by_slot[max(first - 1, 0)][:, h * width * PACK : (h + 1) * width * PACK],
                 )
 
         for t in range(PACK - 1):
@@ -171,12 +180,15 @@ def tile_attend_gsq_x_ts_kernel(tc, xT, wT, y, wt, ts, offs, out):
             if t == 1:
                 woven, planes = weave_views(0)
                 nc.vector.tensor_copy(out=woven, in_=planes)
-                quantise_turned(0)
+                quantise_turned(0, 2)
         last = PACK - 1
         half = SLOTS // 2
-        nc.vector.tensor_copy(
-            out=pairs[1][:, SLOTS : SLOTS + half], in_=tables[last][:].indirect(offsets[:, 0 : half // 16])
-        )
+        quarter = half // 2
+        for first in (0, quarter):
+            nc.vector.tensor_copy(
+                out=pairs[1][:, SLOTS + first : SLOTS + first + quarter],
+                in_=tables[last][:].indirect(offsets[:, first // 16 : (first + quarter) // 16]),
+            )
         nc.scalar.activation(
             out=pairs[1][:, SLOTS + half : 2 * SLOTS],
             in_=tables[last][:].indirect(offsets[:, half // 16 : SLOTS // 16]),
@@ -184,8 +196,11 @@ def tile_attend_gsq_x_ts_kernel(tc, xT, wT, y, wt, ts, offs, out):
         )
         turn_plane(PACK - 1)
         woven, planes = weave_views(1)
-        for first in (0, half // 4):
-            nc.vector.tensor_copy(out=woven[:, first : first + half // 4], in_=planes[:, first : first + half // 4])
+        for first, count in ((0, quarter), (quarter, quarter), (half, half)):
+            part = slice(first // 4, (first + count) // 4)
+            nc.vector.tensor_copy(out=woven[:, part], in_=planes[:, part])
+
+        wd_scales = reuse.tile([P, SLOTS], U8, name="wd_scales", align_bytes=64, offset=TURNED_OFFSET)[:]
 
         def quantise_woven(first):
             nc.vector.quantize_mx(
@@ -230,24 +245,19 @@ def tile_attend_gsq_x_ts_kernel(tc, xT, wT, y, wt, ts, offs, out):
                 x_codes.append(codes[:, n * P : (n + 1) * P])
                 x_scales.append(scales[:, n * P : (n + 1) * P])
 
-        def multiply(j):
-            width = SLOTS
-            banks = []
-            for first in range(0, SLOTS, width):
-                cols = slice(first, first + width)
-                tag = "bank%d" % ((0, 3, 7, 5)[j] + first // half)
-                bank = psum.tile([P, width], F32, name="score_bank%d_%d" % (j, first), tag=tag)
-                nc.tensor.matmul_mx(
-                    out=bank[:],
-                    lhsT=x_codes[j].bitcast(E4M3),
-                    lhsT_scale=x_scales[j],
-                    rhs=wd_codes[:, cols].bitcast(E4M3),
-                    rhs_scale=wd_scales[:, cols],
-                    start=True,
-                    stop=True,
-                )
-                banks.append(bank)
-            score_bank.append(banks)
+        def multiply(j, first, width):
+            if first == 0:
+                score_bank.append(psum.tile([P, SLOTS], F32, name="score_bank%d" % j, tag="bank%d" % (0, 3, 7, 5)[j]))
+            cols = slice(first, first + width)
+            nc.tensor.matmul_mx(
+                out=score_bank[j][:, cols],
+                lhsT=x_codes[j].bitcast(E4M3),
+                lhsT_scale=x_scales[j],
+                rhs=wd_codes[:, cols].bitcast(E4M3),
+                rhs_scale=wd_scales[:, cols],
+                start=True,
+                stop=True,
+            )
 
         def weigh_targets(j):
             place = CAST_OFFSET + 2 * TABLE_BYTES - 4 * SLOTS + 64 if j == 0 else 5 * TABLE_BYTES + j * 4 * SLOTS
@@ -262,23 +272,21 @@ def tile_attend_gsq_x_ts_kernel(tc, xT, wT, y, wt, ts, offs, out):
 
         def scores(j):
             if j == 0:
-                place = CAST_OFFSET + 2 * TABLE_BYTES + 4 * SLOTS - 64
+                place = 4 * TABLE_BYTES + 64
                 score["pair"] = reuse.tile([P, 2, PACK, P], F32, name="score_pair", offset=place)
             if j < 2:
                 scaled = score["pair"][:, j]
             else:
-                scaled = keep.tile([P, PACK, P], F32, name="score%d" % j)
-            words = P // len(score_bank[j])
-            for n, bank in enumerate(score_bank[j]):
-                part = slice(n * words, (n + 1) * words)
-                nc.vector.scalar_tensor_tensor(
-                    out=scaled[:, :, part],
-                    in0=bank[:].rearrange("r (s u) -> r u s", u=PACK),
-                    scalar=wt_cols[:, j : j + 1],
-                    in1=ts_spread[:].rearrange("p (u s) -> p u s", u=PACK)[:, :, part],
-                    op0=MULT,
-                    op1=MULT,
-                )
+                place = SCORE_OFFSET + j * 4 * SLOTS
+                scaled = reuse.tile([P, PACK, P], F32, name="score%d" % j, offset=place)[:]
+            nc.vector.scalar_tensor_tensor(
+                out=scaled,
+                in0=score_bank[j][:].rearrange("r (s u) -> r u s", u=PACK),
+                scalar=wt_cols[:, j : j + 1],
+                in1=ts_spread[:].rearrange("p (u s) -> p u s", u=PACK),
+                op0=MULT,
+                op1=MULT,
+            )
             score[j] = scaled
 
         def turn_targets(j):
@@ -313,10 +321,13 @@ def tile_attend_gsq_x_ts_kernel(tc, xT, wT, y, wt, ts, offs, out):
             h_in[j] = h_tile
 
         h_mx = {}
-        results = []
 
         def quantise_h(j):
-            codes = keep.tile([P, P], U32, name="h_codes%d" % j, align_bytes=64)
+            if j < ROW_TILES - 1:
+                place = 4 * TABLE_BYTES + 64 if j == 0 else SCORE_OFFSET + (j + 1) * 4 * SLOTS
+                codes = reuse.tile([P, P], U32, name="h_codes%d" % j, align_bytes=64, offset=place)
+            else:
+                codes = keep.tile([P, P], U32, name="h_codes%d" % j, align_bytes=64)
             scales = keep.tile([P, P], U8, name="h_scales%d" % j, align_bytes=64)
             nc.vector.quantize_mx(
                 out=codes[:].bitcast(E5M2), scales=scales[:], in_=h_in[j][:].rearrange("s r u -> s (r u)")
@@ -336,33 +347,39 @@ def tile_attend_gsq_x_ts_kernel(tc, xT, wT, y, wt, ts, offs, out):
                 start=True,
                 stop=True,
             )
-            result = keep.tile([P, width], F32, name="result%d_%d" % (j, first))
-            written = result[:].rearrange("r (h p t) -> r h p t", p=P // 2, t=PACK)
-            read = bank[:].rearrange("r (h t p) -> r h p t", p=P // 2, t=PACK)
-            if on_vector:
-                nc.vector.tensor_copy(out=written, in_=read)
-            else:
-                nc.scalar.copy(out=written, in_=read)
-            queue = nc.scalar if first > 0 else nc.sync
-            queue.dma_start(out=out[0, j * P : (j + 1) * P, cols], in_=result[:])
-            results.append(result)
+            piece = FEATURES // 2 if j == 0 else width
+            for start in range(0, width, piece):
+                result = keep.tile([P, piece], F32, name="result%d_%d" % (j, first + start))
+                written = result[:].rearrange("r (h p t) -> r h p t", p=P // 2, t=PACK)
+                read = bank[:, start : start + piece].rearrange("r (h t p) -> r h p t", p=P // 2, t=PACK)
+                if on_vector:
+                    nc.vector.tensor_copy(out=written, in_=read)
+                else:
+                    nc.scalar.copy(out=written, in_=read)
+                queue = nc.scalar if first > 0 else nc.sync
+                queue.dma_start(
+                    out=out[0, j * P : (j + 1) * P, first + start : first + start + piece], in_=result[:]
+                )
 
+        copy_turned(2)
         cast_x(0)
         quantise_woven(0)
         quantise_x(0)
+        multiply(0, 0, half)
         quantise_woven(half)
-        multiply(0)
+        multiply(0, half, half)
         cast_x(1)
-        quantise_x(1)
-        multiply(1)
         cast_x(2)
-        cast_x(3)
-        quantise_x(2)
-        scores(0)
-        multiply(2)
-        multiply(3)
-        copy_turned(2)
         copy_turned(3)
+        quantise_x(1)
+        multiply(1, 0, SLOTS)
+        cast_x(3)
+        quantise_turned(2, 1)
+        quantise_x(2)
+        quantise_turned(3, 1)
+        scores(0)
+        multiply(2, 0, SLOTS)
+        multiply(3, 0, SLOTS)
         weigh_targets(0)
         scores(1)
         turn_targets(0)
@@ -371,24 +388,20 @@ def tile_attend_gsq_x_ts_kernel(tc, xT, wT, y, wt, ts, offs, out):
         weigh_targets(1)
         turn_targets(1)
         turn_scores(1)
-        scale_gradient(0)
         scores(3)
-        quantise_turned(1)
         weigh_targets(2)
         weigh_targets(3)
+        scale_gradient(0)
         turn_targets(2)
         turn_scores(2)
-        quantise_h(0)
-        finish(0, 0, FEATURES, 1, False)
-        scale_gradient(1)
         turn_targets(3)
         turn_scores(3)
-        quantise_h(1)
-        finish(1, 0, FEATURES, 3, False)
-        scale_gradient(2)
-        scale_gradient(3)
-        quantise_h(2)
-        finish(2, 0, FEATURES, 7, False)
+        for j in range(1, ROW_TILES):
+            scale_gradient(j)
+            quantise_h(j - 1)
+            if j < ROW_TILES - 1:
+                finish(j - 1, 0, FEATURES, (1, 3)[j - 1], False)
         quantise_h(3)
-        finish(3, 0, FEATURES // 2, 5, True)
-        finish(3, FEATURES // 2, FEATURES // 2, 1, False)
+        for j, banks in ((2, (7, 2)), (3, (5, 4))):
+            finish(j, 0, FEATURES // 2, banks[0], True)
+            finish(j, FEATURES // 2, FEATURES // 2, banks[1], False)

@@ -235,15 +235,12 @@ def tile_attend_gsq_x_ts_kernel(tc, xT, wT, y, wt, ts, offs, out):
             )
 
         def quantise_x(j):
-            count = 1 if j < 2 else 2
-            codes = keep.tile([P, count * P], U32, name="x_codes%d" % j, align_bytes=64)
-            scales = keep.tile([P, count * P], U8, name="x_scales%d" % j, align_bytes=64)
-            nc.vector.quantize_mx(
-                out=codes[:].bitcast(E4M3), scales=scales[:], in_=x_ins[j][:].rearrange("p c t -> p (c t)")
-            )
-            for n in range(count):
-                x_codes.append(codes[:, n * P : (n + 1) * P])
-                x_scales.append(scales[:, n * P : (n + 1) * P])
+            codes = keep.tile([P, P], U32, name="x_codes%d" % j, align_bytes=64)
+            scales = keep.tile([P, P], U8, name="x_scales%d" % j, align_bytes=64)
+            x_in = x_ins[min(j, 2)][:, (j // 3) * P : (j // 3 + 1) * P, :]
+            nc.vector.quantize_mx(out=codes[:].bitcast(E4M3), scales=scales[:], in_=x_in.rearrange("p c t -> p (c t)"))
+            x_codes.append(codes[:])
+            x_scales.append(scales[:])
 
         def multiply(j, first, width):
             if first == 0:
@@ -334,7 +331,7 @@ def tile_attend_gsq_x_ts_kernel(tc, xT, wT, y, wt, ts, offs, out):
             )
             h_mx[j] = (codes, scales)
 
-        def finish(j, first, width, tag, on_vector):
+        def product(j, first, width, tag):
             codes, scales = h_mx[j]
             cols = slice(first, first + width)
             bank = psum.tile([P, width], F32, name="out_bank%d_%d" % (j, first), tag="bank%d" % tag)
@@ -347,19 +344,26 @@ def tile_attend_gsq_x_ts_kernel(tc, xT, wT, y, wt, ts, offs, out):
                 start=True,
                 stop=True,
             )
-            piece = FEATURES // 2 if j == 0 else width
-            for start in range(0, width, piece):
-                result = keep.tile([P, piece], F32, name="result%d_%d" % (j, first + start))
-                written = result[:].rearrange("r (h p t) -> r h p t", p=P // 2, t=PACK)
-                read = bank[:, start : start + piece].rearrange("r (h t p) -> r h p t", p=P // 2, t=PACK)
-                if on_vector:
-                    nc.vector.tensor_copy(out=written, in_=read)
-                else:
-                    nc.scalar.copy(out=written, in_=read)
-                queue = nc.scalar if first > 0 else nc.sync
-                queue.dma_start(
-                    out=out[0, j * P : (j + 1) * P, first + start : first + start + piece], in_=result[:]
-                )
+            return bank
+
+        def copy_out(copy, result, read):
+            copy(
+                out=result.rearrange("r (p t) -> r p t", t=PACK),
+                in_=read.rearrange("r (t p) -> r p t", t=PACK),
+            )
+
+        def finish_in_turn(j, tag):
+            bank = product(j, 0, FEATURES, tag)
+            for first in (0, half):
+                result = keep.tile([P, half], F32, name="result%d_%d" % (j, first))
+                copy_out(nc.scalar.copy, result[:], bank[:, first : first + half])
+                nc.sync.dma_start(out=out[0, j * P : (j + 1) * P, first : first + half], in_=result[:])
+
+        def finish_side_by_side(j, tags):
+            result = keep.tile([P, FEATURES], F32, name="result%d" % j)
+            copy_out(nc.vector.tensor_copy, result[:, 0:half], product(j, 0, half, tags[0])[:])
+            copy_out(nc.scalar.copy, result[:, half:FEATURES], product(j, half, half, tags[1])[:])
+            nc.sync.dma_start(out=out[0, j * P : (j + 1) * P, :], in_=result[:])
 
         copy_turned(2)
         cast_x(0)
@@ -376,6 +380,7 @@ def tile_attend_gsq_x_ts_kernel(tc, xT, wT, y, wt, ts, offs, out):
         cast_x(3)
         quantise_turned(2, 1)
         quantise_x(2)
+        quantise_x(3)
         quantise_turned(3, 1)
         scores(0)
         multiply(2, 0, SLOTS)
@@ -400,8 +405,7 @@ def tile_attend_gsq_x_ts_kernel(tc, xT, wT, y, wt, ts, offs, out):
             scale_gradient(j)
             quantise_h(j - 1)
             if j < ROW_TILES - 1:
-                finish(j - 1, 0, FEATURES, (1, 3)[j - 1], False)
+                finish_in_turn(j - 1, (1, 3)[j - 1])
         quantise_h(3)
-        for j, banks in ((2, (7, 2)), (3, (5, 4))):
-            finish(j, 0, FEATURES // 2, banks[0], True)
-            finish(j, FEATURES // 2, FEATURES // 2, banks[1], False)
+        finish_side_by_side(2, (7, 2))
+        finish_side_by_side(3, (5, 4))

@@ -229,9 +229,10 @@ def tile_attend_gsq_x_ts_kernel(tc, xT, wT, y, wt, ts, offs, out):
                 )
             x_in = x_ins[min(j, 2)][:, (j // 3) * P : (j // 3 + 1) * P, :]
             copy = nc.vector.tensor_copy if j == 3 else nc.scalar.copy
+            run = 4 if j == 3 else 2
             copy(
-                out=x_in.rearrange("p (c i) t -> p c t i", i=4),
-                in_=x_raw[j].rearrange("p t (c i) -> p c t i", i=4),
+                out=x_in.rearrange("p (c i) t -> p c t i", i=run),
+                in_=x_raw[j].rearrange("p t (c i) -> p c t i", i=run),
             )
 
         def quantise_x(j):

from contextlib import ExitStack

import concourse.mybir as mybir
from concourse.masks import make_identity

F32 = mybir.dt.float32
BF16 = mybir.dt.bfloat16
U32 = mybir.dt.uint32
U16 = mybir.dt.uint16
U8 = mybir.dt.uint8
E4M3 = mybir.dt.float8_e4m3fn_x4
E5M2 = mybir.dt.float8_e5m2_x4
MULT = mybir.AluOpType.mult
COPY = mybir.ActivationFunctionType.Copy

P = 128
PACK = 4
SLOTS = 512
ITEMS = 2048
FEATURES = 512
ROWS = 512
ROW_TILES = ROWS // P
TILES_PER_LOAD = 2
ZEROED_BY_VECTOR = 1536
TS_ROW = P - 1
WT_ROW = 60

TABLE_BYTES = 4 * ITEMS
Y0_OFFSET = 7 * TABLE_BYTES
WOVEN_OFFSET = 8 * TABLE_BYTES
CAST_OFFSET = 9 * TABLE_BYTES
TURNED_OFFSET = 12 * TABLE_BYTES
SCORE_OFFSET = 13 * TABLE_BYTES

FLOPS = 2 * 2 * ROWS * SLOTS * FEATURES


def tile_attend_gsq_x_ts_kernel(tc, xT, wT, y, wt, ts, offs, out):
    nc = tc.nc
    with ExitStack() as ctx:
        keep = ctx.enter_context(tc.tile_pool(name="keep", bufs=1))
        reuse = ctx.enter_context(tc.tile_pool(name="reuse", bufs=1))
        psum = ctx.enter_context(tc.psum_pool(name="psum", bufs=1))

        wt_rows = reuse.tile([P, P], F32, name="wt_rows", offset=Y0_OFFSET)
        nc.gpsimd.memset(wt_rows[0:WT_ROW, :], 0.0)
        nc.gpsimd.memset(wt_rows[WT_ROW + ROW_TILES : P, :], 0.0)
        ts_table = reuse.tile([P, ITEMS], F32, name="ts_table", offset=4 * TABLE_BYTES)
        nc.vector.memset(ts_table[0:TS_ROW, 0:ZEROED_BY_VECTOR].bitcast(U32), 0)
        nc.gpsimd.memset(ts_table[0:TS_ROW, ZEROED_BY_VECTOR:ITEMS], 0.0)
        ident_f32 = keep.tile([P, P], F32, name="ident_f32")
        make_identity(nc, ident_f32[:])

        offsets = keep.tile([P, SLOTS // 16], U16, name="offsets")
        w_planes = wT.rearrange("(p t) c -> p t c", t=PACK)
        tables = []
        for t in range(PACK):
            tables.append(reuse.tile([P, ITEMS], F32, name="table%d" % t, offset=t * TABLE_BYTES))
        for t in range(PACK):
            nc.sync.dma_start(out=tables[t][:], in_=w_planes[:, t, :])
            if t == 0:
                nc.sync.dma_start(offsets[:], offs)
                nc.scalar.dma_start(out=ts_table[TS_ROW : TS_ROW + 1, :], in_=ts[0:1, :])
                nc.scalar.dma_start(
                    out=wt_rows[WT_ROW : WT_ROW + ROW_TILES, :], in_=wt[0].rearrange("(j p) o -> j (p o)", p=P)
                )

        x_planes = xT[0].rearrange("(p t) r -> p t r", t=PACK)
        x_raw = []
        y_raw = []

        def load_x(half):
            width = TILES_PER_LOAD * P
            place = (WOVEN_OFFSET - TABLE_BYTES // 2, 4 * TABLE_BYTES)[half]
            x_half = reuse.tile([P, PACK, width], F32, name="x_raw%d" % half, offset=place)
            nc.sync.dma_start(out=x_half[:], in_=x_planes[:, :, half * width : (half + 1) * width])
            for jj in range(TILES_PER_LOAD):
                x_raw.append(x_half[:, :, jj * P : (jj + 1) * P])

        def load_y(j):
            place = 5 * TABLE_BYTES - 4 * SLOTS if j == 0 else 2 * TABLE_BYTES + j * 4 * SLOTS
            y_tile = reuse.tile([P, SLOTS], F32, name="y_raw%d" % j, offset=place)
            nc.sync.dma_start(out=y_tile[:], in_=y[0, j * P : (j + 1) * P, :])
            y_raw.append(y_tile[:])

        ts_row = keep.tile([P, SLOTS], F32, name="ts_row")
        nc.vector.tensor_copy(out=ts_row[:], in_=ts_table[:].indirect(offsets[:]))
        ts_dealt = keep.tile([P, SLOTS], F32, name="ts_dealt")
        nc.scalar.activation(
            out=ts_dealt[:].rearrange("p (u s) -> p s u", u=PACK),
            in_=ts_row[:].rearrange("p (s u) -> p s u", u=PACK),
            func=COPY,
            scale=-1.0,
        )
        ts_bank = psum.tile([P, PACK, P], F32, name="ts_bank", tag="bank4")
        for u in range(PACK):
            nc.tensor.transpose(ts_bank[:, u, :], ts_dealt[:, u * P : (u + 1) * P], ident_f32[:])
        ts_wide = keep.tile([P, PACK, P], F32, name="ts_wide")
        nc.scalar.copy(out=ts_wide[:], in_=ts_bank[:, :, TS_ROW : TS_ROW + 1].to_broadcast([P, PACK, P]))
        ts_cols = keep.tile([P, PACK], F32, name="ts_cols")
        nc.scalar.copy(out=ts_cols[:], in_=ts_bank[:, :, TS_ROW])
        spread_bank = psum.tile([P, PACK, P], F32, name="spread_bank", tag="bank6")
        for u in range(PACK):
            nc.tensor.transpose(spread_bank[:, u, :], ts_wide[:, u, :], ident_f32[:])
        ts_spread = keep.tile([P, SLOTS], F32, name="ts_spread")
        nc.scalar.copy(out=ts_spread[:], in_=spread_bank[:].rearrange("p u s -> p (u s)"))

        wt_bank = psum.tile([P, P], F32, name="wt_bank", tag="bank5")
        nc.tensor.transpose(wt_bank[:], wt_rows[:], ident_f32[:])
        wt_cols = keep.tile([P, ROW_TILES], F32, name="wt_cols")
        nc.scalar.copy(out=wt_cols[:], in_=wt_bank[:, WT_ROW : WT_ROW + ROW_TILES])

        w_by_d = reuse.tile([P, SLOTS, PACK], BF16, name="w_by_d", align_bytes=64, offset=WOVEN_OFFSET)
        pairs = [
            keep.tile([P, 2 * SLOTS], BF16, name="pair0"),
            reuse.tile([P, 2 * SLOTS], BF16, name="pair1", offset=4 * TABLE_BYTES + TABLE_BYTES // 2),
        ]
        wn_codes = keep.tile([P, FEATURES], U32, name="wn_codes", align_bytes=64)
        w_scales = reuse.tile([P, SLOTS], U8, name="w_scales", align_bytes=64, offset=2 * TABLE_BYTES)
        wn_scales = w_scales[:]
        wd_codes = keep.tile([P, SLOTS], U32, name="wd_codes", align_bytes=64)
        w_by_slot = []

        def gather_plane(t):
            plane = pairs[t // 2][:, (t % 2) * SLOTS : (t % 2 + 1) * SLOTS]
            nc.vector.tensor_copy(out=plane, in_=tables[t][:].indirect(offsets[:]))

        def weave_views(pair):
            woven = w_by_d[:, :, 2 * pair : 2 * pair + 2].rearrange("p (c i) t -> p c t i", i=4)
            planes = pairs[pair][:].rearrange("p (t c i) -> p c t i", t=2, i=4)
            return woven, planes

        turn_banks = []

        def turn_plane(t):
            words = pairs[t // 2][:].bitcast(F32)
            first = (t % 2) * (SLOTS // 2)
            turn_bank = psum.tile([P, 2, P], F32, name="turn_bank%d" % t, tag="bank%d" % (3, 2, 6, 2)[t])
            for v in range(2):
                nc.tensor.transpose(turn_bank[:, v, :], words[:, first + v : first + SLOTS // 2 : 2], ident_f32[:])
            turn_banks.append(turn_bank)

        def copy_turned(t):
            if t == 0:
                w_by_slot.append(
                    reuse.tile([P, 2 * P * PACK], BF16, name="w_by_slot0", align_bytes=64, offset=TURNED_OFFSET)
                )
            if t < 2:
                words = w_by_slot[0][:].bitcast(F32).rearrange("s (h t p v) -> s t h p v", h=2, t=2, v=2)[:, t]
            else:
                place = (3 * TABLE_BYTES, 4 * TABLE_BYTES - 2 * SLOTS + 64)[t - 2]
                w_by_slot.append(
                    reuse.tile([P, P * PACK], BF16, name="w_by_slot%d" % t, align_bytes=64, offset=place)
                )
                words = w_by_slot[t - 1][:].bitcast(F32).rearrange("s (h p v) -> s h p v", h=2, v=2)
            nc.scalar.copy(out=words, in_=turn_banks[t][:].rearrange("s v (h p) -> s h p v", h=2))

        def quantise_turned(first, count):
            width = count * P // 2
            for h in range(2):
                start = (PACK * h + first) * P // 2
                nc.vector.quantize_mx(
                    out=wn_codes[:, start : start + width].bitcast(E4M3),
                    scales=wn_scales[:, start : start + width],
                    in_=w_by_slot[max(first - 1, 0)][:, h * width * PACK : (h + 1) * width * PACK],
                )

        for t in range(PACK - 1):
            gather_plane(t)
            if t < 2:
                load_x(t)
            if t == 1:
                load_y(0)
            if t == 2:
                for j in range(1, ROW_TILES):
                    load_y(j)
            turn_plane(t)
            if t < 2:
                copy_turned(t)
            if t == 1:
                woven, planes = weave_views(0)
                nc.vector.tensor_copy(out=woven, in_=planes)
                quantise_turned(0, 2)
        last = PACK - 1
        half = SLOTS // 2
        quarter = half // 2
        for first in (0, quarter):
            nc.vector.tensor_copy(
                out=pairs[1][:, SLOTS + first : SLOTS + first + quarter],
                in_=tables[last][:].indirect(offsets[:, first // 16 : (first + quarter) // 16]),
            )
        nc.scalar.activation(
            out=pairs[1][:, SLOTS + half : 2 * SLOTS],
            in_=tables[last][:].indirect(offsets[:, half // 16 : SLOTS // 16]),
            func=COPY,
        )
        turn_plane(PACK - 1)
        woven, planes = weave_views(1)
        for first, count in ((0, quarter), (quarter, quarter), (half, half)):
            part = slice(first // 4, (first + count) // 4)
            nc.vector.tensor_copy(out=woven[:, part], in_=planes[:, part])

        wd_scales = reuse.tile([P, SLOTS], U8, name="wd_scales", align_bytes=64, offset=TURNED_OFFSET)[:]

        def quantise_woven(first):
            nc.vector.quantize_mx(
                out=wd_codes[:, first : first + half].bitcast(E4M3),
                scales=wd_scales[:, first : first + half],
                in_=w_by_d[:, first : first + half, :].rearrange("p c t -> p (c t)"),
            )

        x_codes = []
        x_scales = []
        score_bank = []
        grad_bank = []
        y_neg = []
        score = {}
        h_in = {}

        x_ins = []

        def cast_x(j):
            if j < 3:
                count = 1 if j < 2 else 2
                x_ins.append(
                    reuse.tile(
                        [P, count * P, PACK], BF16, name="x_in%d" % j, align_bytes=64, offset=CAST_OFFSET + j * TABLE_BYTES
                    )
                )
            x_in = x_ins[min(j, 2)][:, (j // 3) * P : (j // 3 + 1) * P, :]
            copy = nc.vector.tensor_copy if j == 3 else nc.scalar.copy
            run = 4 if j == 3 else 2
            copy(
                out=x_in.rearrange("p (c i) t -> p c t i", i=run),
                in_=x_raw[j].rearrange("p t (c i) -> p c t i", i=run),
            )

        def quantise_x(j):
            codes = keep.tile([P, P], U32, name="x_codes%d" % j, align_bytes=64)
            scales = keep.tile([P, P], U8, name="x_scales%d" % j, align_bytes=64)
            x_in = x_ins[min(j, 2)][:, (j // 3) * P : (j // 3 + 1) * P, :]
            nc.vector.quantize_mx(out=codes[:].bitcast(E4M3), scales=scales[:], in_=x_in.rearrange("p c t -> p (c t)"))
            x_codes.append(codes[:])
            x_scales.append(scales[:])

        def multiply(j, first, width):
            if first == 0:
                score_bank.append(psum.tile([P, SLOTS], F32, name="score_bank%d" % j, tag="bank%d" % (0, 3, 7, 5)[j]))
            cols = slice(first, first + width)
            nc.tensor.matmul_mx(
                out=score_bank[j][:, cols],
                lhsT=x_codes[j].bitcast(E4M3),
                lhsT_scale=x_scales[j],
                rhs=wd_codes[:, cols].bitcast(E4M3),
                rhs_scale=wd_scales[:, cols],
                start=True,
                stop=True,
            )

        def weigh_targets(j):
            place = CAST_OFFSET + 2 * TABLE_BYTES - 4 * SLOTS + 64 if j == 0 else 5 * TABLE_BYTES + j * 4 * SLOTS
            target = reuse.tile([P, PACK, P], F32, name="y_neg%d" % j, offset=place)
            nc.scalar.activation(
                out=target[:].rearrange("r u s -> r s u"),
                in_=y_raw[j].rearrange("r (s u) -> r s u", u=PACK),
                func=COPY,
                scale=wt_cols[:, j : j + 1],
            )
            y_neg.append(target)

        def scores(j):
            if j == 0:
                place = 4 * TABLE_BYTES + 64
                score["pair"] = reuse.tile([P, 2, PACK, P], F32, name="score_pair", offset=place)
            if j < 2:
                scaled = score["pair"][:, j]
            else:
                place = SCORE_OFFSET + j * 4 * SLOTS
                scaled = reuse.tile([P, PACK, P], F32, name="score%d" % j, offset=place)[:]
            nc.vector.scalar_tensor_tensor(
                out=scaled,
                in0=score_bank[j][:].rearrange("r (s u) -> r u s", u=PACK),
                scalar=wt_cols[:, j : j + 1],
                in1=ts_spread[:].rearrange("p (u s) -> p u s", u=PACK),
                op0=MULT,
                op1=MULT,
            )
            score[j] = scaled

        def turn_targets(j):
            bank = psum.tile([P, PACK, P], F32, name="grad_bank%d" % j, tag="bank%d" % (4, 0, 2, 6)[j])
            grad_bank.append(bank)
            for u in range(PACK):
                nc.tensor.matmul(
                    bank[:, u, :], lhsT=y_neg[j][:, u, :], rhs=ident_f32[:], start=(u == 0), stop=False, is_transpose=True
                )

        def turn_scores(j):
            bank = grad_bank[j]
            for u in range(PACK):
                nc.tensor.matmul(
                    bank[:, u, :],
                    lhsT=score[j][:, u, :],
                    rhs=ident_f32[:],
                    start=False,
                    stop=(u == PACK - 1),
                    is_transpose=True,
                )

        def scale_gradient(j):
            bank = grad_bank[j]
            h_tile = keep.tile([P, P, PACK], BF16, name="h_in%d" % j, align_bytes=64)
            nc.vector.tensor_tensor(
                out=h_tile[:],
                in0=bank[:].rearrange("s u r -> s r u"),
                in1=ts_cols[:].unsqueeze(1).to_broadcast([P, P, PACK]),
                op=MULT,
            )
            h_in[j] = h_tile

        h_mx = {}

        def quantise_h(j):
            if j < ROW_TILES - 1:
                place = 4 * TABLE_BYTES + 64 if j == 0 else SCORE_OFFSET + (j + 1) * 4 * SLOTS
                codes = reuse.tile([P, P], U32, name="h_codes%d" % j, align_bytes=64, offset=place)
            else:
                codes = keep.tile([P, P], U32, name="h_codes%d" % j, align_bytes=64)
            scales = keep.tile([P, P], U8, name="h_scales%d" % j, align_bytes=64)
            nc.vector.quantize_mx(
                out=codes[:].bitcast(E5M2), scales=scales[:], in_=h_in[j][:].rearrange("s r u -> s (r u)")
            )
            h_mx[j] = (codes, scales)

        def product(j, first, width, tag):
            codes, scales = h_mx[j]
            cols = slice(first, first + width)
            bank = psum.tile([P, width], F32, name="out_bank%d_%d" % (j, first), tag="bank%d" % tag)
            nc.tensor.matmul_mx(
                out=bank[:],
                lhsT=codes[:].bitcast(E5M2),
                lhsT_scale=scales[:],
                rhs=wn_codes[:, cols].bitcast(E4M3),
                rhs_scale=wn_scales[:, cols],
                start=True,
                stop=True,
            )
            return bank

        def copy_out(copy, result, read):
            copy(
                out=result.rearrange("r (p t) -> r p t", t=PACK),
                in_=read.rearrange("r (t p) -> r p t", t=PACK),
            )

        def finish_in_turn(j, tag):
            bank = product(j, 0, FEATURES, tag)
            for first in (0, half):
                result = keep.tile([P, half], F32, name="result%d_%d" % (j, first))
                copy_out(nc.scalar.copy, result[:], bank[:, first : first + half])
                nc.sync.dma_start(out=out[0, j * P : (j + 1) * P, first : first + half], in_=result[:])

        def finish_side_by_side(j, tags):
            result = keep.tile([P, FEATURES], F32, name="result%d" % j)
            copy_out(nc.vector.tensor_copy, result[:, 0:half], product(j, 0, half, tags[0])[:])
            copy_out(nc.scalar.copy, result[:, half:FEATURES], product(j, half, half, tags[1])[:])
            nc.sync.dma_start(out=out[0, j * P : (j + 1) * P, :], in_=result[:])

        copy_turned(2)
        cast_x(0)
        quantise_woven(0)
        quantise_x(0)
        multiply(0, 0, half)
        quantise_woven(half)
        multiply(0, half, half)
        cast_x(1)
        cast_x(2)
        copy_turned(3)
        quantise_x(1)
        multiply(1, 0, SLOTS)
        cast_x(3)
        quantise_turned(2, 1)
        quantise_x(2)
        quantise_x(3)
        quantise_turned(3, 1)
        scores(0)
        multiply(2, 0, SLOTS)
        multiply(3, 0, SLOTS)
        weigh_targets(0)
        scores(1)
        turn_targets(0)
        turn_scores(0)
        scores(2)
        weigh_targets(1)
        turn_targets(1)
        turn_scores(1)
        scores(3)
        weigh_targets(2)
        weigh_targets(3)
        scale_gradient(0)
        turn_targets(2)
        turn_scores(2)
        turn_targets(3)
        turn_scores(3)
        for j in range(1, ROW_TILES):
            scale_gradient(j)
            quantise_h(j - 1)
            if j < ROW_TILES - 1:
                finish_in_turn(j - 1, (1, 3)[j - 1])
        quantise_h(3)
        finish_side_by_side(2, (7, 2))
        finish_side_by_side(3, (5, 4))
